import numpy as np, ml_dtypes
CORES = [3,11,19,27,35,43,51,59]
N = 8
BF = ml_dtypes.bfloat16
V, TY, LN, SL, RT, RO, ST = 2048, 1024, 512, 128, 64, 3, 896
WT = 1 + 10 * np.arange(16)
def cand(u):
    return ((u * u >> 5) + u + np.arange(16)[:, None] * (2 * u + 1)) & (V - 1)
def pack(w, x, q, s, h, v, t):
    i = lambda a, n: np.ascontiguousarray(a).reshape(N, -1, n).astype(np.int32)
    b = lambda a, n: np.ascontiguousarray(a).reshape(N, -1, n).astype(np.float32).astype(BF)
    return {"wd": i(w, V), "xs": b(x, V), "rq": i(q, TY), "sg": b(s, TY), "hy": i(h, V), "vf": i(v, V), "th": i(t, 1)}
def world(rng, A, top, size, twin, noise, pw, wrong, harm):
    w = np.zeros((N, 8, 16, V), np.int64); x = w.copy(); q = np.zeros((N, 8, 16, TY), np.int64); s = q.copy(); h = np.zeros((N, 8, V), np.int64); tt = h.copy()
    for r in range(N):
        for g in range(8):
            live = rng.permutation(TY)[:A]
            sa = rng.integers(0, top + 1, (16, TY)) >> rng.integers(0, size + 1, (1, TY))
            sa[:, live[1::2]] = np.clip(sa[:, live[0::2]] + rng.integers(-twin, twin + 1, (16, A // 2)), 0, 255)
            qa = np.where(rng.random((16, TY)) < rng.random((1, TY)), live[(A * rng.random((16, TY)) ** pw).astype(np.int64)], TY)
            k = rng.permutation(np.concatenate([np.arange(A), (A * rng.random(V - A) ** pw).astype(np.int64)]))
            o = np.argsort(k, kind="stable"); n = np.bincount(k, minlength=A); b = np.add.accumulate(n) - n
            back = np.zeros(TY + 1, np.int64); back[live] = np.arange(A)
            need = qa[:, live[k]]; kk = back[need]
            wa = o[b[kk] + (n[kk] * rng.random((16, V)) ** pw).astype(np.int64)]
            p = rng.choice(np.array([0.0, 0.0, 0.0, 0.0, 0.0, 0.0, 0.15, 0.15, 0.15, 0.5]), V) * harm
            wa = np.where((need == TY) | (rng.random((16, V)) < p), rng.integers(0, V, (16, V)), wa)
            off = np.where(rng.random(V) < 0.5, live[rng.integers(0, A, V)], rng.integers(0, TY, V))
            h[r, g] = np.where(rng.random(V) < wrong[r, g], off, live[k]); tt[r, g] = live[k]
            x[r, g] = np.clip(sa[:, live[k]] + rng.integers(-noise, noise + 1, (16, V)), 0, 255)
            w[r, g], q[r, g], s[r, g] = wa, qa, sa
    return w, x, q, s, h, tt
def setup_inputs(rng):
    wrong = rng.choice(np.array([0.004, 0.02, 0.06, 0.15]), (N, 8))
    w, x, q, s, h, tt = world(rng, min(V, TY) // 2, 255, 0, 3, 4, 1, wrong, 1.0)
    v = rng.random((N, 8, V)) < rng.choice(np.array([0.02, 0.2, 0.5, 0.85]), (N, 8, 1))
    t = 40 + (1200 * rng.random((N, 8, 16)) ** 2).astype(np.int64)
    return pack(w, x, q, s, h, v, t)
def setup_inputs_spread(rng):
    w, x, q, s, h, tt = world(rng, min(V, TY) // 2, 255, 7, 2, 4, 3, 0.2 * rng.random((N, 8)), 1.0)
    v = rng.random((N, 8, V)) < rng.random((N, 8, 1))
    t = np.minimum(np.exp2(12 * rng.random((N, 8, 16))).astype(np.int64) - 1, 4080)
    return pack(w, x, q, s, h, v, t)
def setup_inputs_ties(rng):
    w, x, q, s, h, tt = world(rng, 8, 150, 0, 0, 0, 1, rng.choice(np.array([0.1, 0.3, 0.5]), (N, 8)), 0.5)
    near = np.array([49, 50, 51])
    x = np.take_along_axis(s, np.broadcast_to(tt[:, :, None, :], (N, 8, 16, V)), 3)
    x = x + (np.arange(16)[:, None] == rng.integers(0, 16, (N, 8, 1, V))) * rng.choice(near, (N, 8, 1, V))
    v = rng.random((N, 8, V)) < rng.choice(np.array([0.1, 0.4, 0.6]), (N, 8, 1))
    return pack(w, x, q, s, h, v, rng.choice(near, (N, 8, 16)))
def setup_inputs_ends(rng):
    def two(lo, hi, *sh): return np.where(rng.random(sh) < 0.5, lo, hi)
    x = np.where(rng.random((N, 8, 1, V)) < 0.5, two(0, 255, N, 8, 1, V), two(0, 255, N, 8, 16, V))
    s = np.where(rng.random((N, 8, 1, TY)) < 0.5, two(0, 255, N, 8, 1, TY), two(0, 255, N, 8, 16, TY))
    h = np.where(rng.random((N, 8, V)) < 0.9, two(0, TY - 1, N, 8, V), rng.integers(0, TY, (N, 8, V)))
    v = (rng.random((N, 8, V)) < 0.4).astype(np.int64)
    w = np.where(rng.random((N, 8, 16, V)) < 0.8, two(0, V - 1, N, 8, 16, V), rng.integers(0, V, (N, 8, 16, V)))
    q = np.where(rng.random((N, 8, 16, TY)) < 0.7, two(0, TY, N, 8, 16, TY), TY - 1)
    for c in (0, TY - 1): q[..., c] = np.where(rng.random((N, 8, 16)) < 0.85, two(0, TY - 1, N, 8, 16), TY)
    z = np.stack([rng.permutation(np.array([2, 3, 4, 5, 6, 8, 12, 16])) for r in range(N)]); z[:, 7] = 5
    t = np.where(np.argsort(rng.random((N, 8, 16)), axis=-1) < z[..., None], 0, 4080)
    c = cand(np.array([(255 * 1216) & (V - 1)]))[:, 0]
    v[:, 7, 0] = 1; v[:, 7, V - 1] = 0; v[:, 7, c[:2]] = 0; v[:, 7, c[2]] = 1; v[:, 7, c[15]] = 1
    x[:, 7] = np.where(v[:, 7] == 1, 0, 255)[:, None, :]
    lo = two(0, 255, N, 8, 1); lo[:, 7] = 0
    x[..., 0] = lo; x[..., V - 1] = 255 - lo; s[..., 0] = 255 - lo
    s[..., TY - 1] = np.where(rng.random((N, 8, 1)) < 0.5, lo, 255 - lo); s[:, 7, :, TY - 1] = 0
    h[..., 0] = TY - 1; h[..., V - 1] = 0
    q[0, :, 0] = TY; t[0] = 4080; t[0, :, 0] = 0
    return pack(w, x, q, s, h, v, t)
def setup_inputs_corners(rng):
    w0 = np.zeros((N, 8, 16, V), np.int64); x0 = w0.copy(); q0 = np.zeros((N, 8, 16, TY), np.int64); s0 = q0.copy(); h0 = np.zeros((N, 8, V), np.int64); v0 = h0.copy()
    all_ = V - 16
    plan_u = (all_, LN, LN + 1, LN - 1, 1, 0, all_, all_); plan_p = (SL, SL + 1, SL - 1, LN, 1, 0, 0, SL); plan_t = (RT, RT + 1, RT - 1, 0, 0, 0, LN, RT)
    for r in range(N):
        for g in range(8):
            live = rng.permutation(TY)[:32]; s = rng.integers(0, 256, (16, TY)); s[:, live[1::2]] = s[:, live[0::2]]
            q = np.where(rng.random((16, TY)) < 0.6, live[rng.integers(0, 32, (16, TY))], TY)
            q[np.array([0, 3, 7, 11])] = live[rng.integers(0, 32, (4, TY))]; q[15, live] = live
            z = 1 + rng.permutation(V - 2)[:16]; reg = np.setdiff1d(np.arange(V), z)
            k = rng.permutation(np.concatenate([np.arange(32), rng.integers(0, 32, V - 48)]))
            o = np.argsort(k, kind="stable"); n = np.bincount(k, minlength=32); b = np.add.accumulate(n) - n
            back = np.zeros(TY + 1, np.int64); back[live] = np.arange(32)
            pairs = np.arange(16)
            h = np.zeros(V, np.int64); h[reg] = live[k]; h[z] = live[(2 * pairs + 2) % 32]
            x = np.zeros((16, V), np.int64); x[:, reg] = np.clip(s[:, live[k]] + rng.integers(-3, 4, (16, V - 16)), 0, 255); x[:, z] = s[:, live[2 * pairs]]
            w = rng.integers(0, V, (16, V)); need = q[:, h[reg]]; kk = back[need]
            wr = np.where(need == TY, w[:, reg], reg[o[b[kk] + (n[kk] * rng.random(kk.shape)).astype(np.int64)]])
            wr[15] = np.where(rng.random(V - 16) < 0.5, reg, wr[15])
            for e in (0, V - 17): wr = np.where((need < TY) & (kk == k[e]) & (rng.random(kk.shape) < 0.3), reg[e], wr)
            w[:, reg] = wr
            if r == 0: nu, n1, n2 = plan_u[g], plan_p[g], plan_t[g]
            else:
                nu = int(rng.choice(np.array([0, 1, LN - 1, LN, LN, LN + 1, all_, all_])))
                n1 = int(rng.choice(np.array([0, 1, SL - 1, SL, SL + 1, LN - RT - 1]))); n2 = int(rng.choice(np.array([0, 1, RT - 1, RT, RT + 1, LN])))
            on = np.sort(rng.permutation(reg)[:nu]); v = np.ones(V, np.int64); v[on] = 0
            la = rng.permutation(on[:LN]); m = len(la); n1 = min(n1, m); n2 = min(n2, m - n1); n3 = min(m - n1 - n2, int(rng.integers(0, 40)))
            nd = np.zeros(m, np.int64); nd[:n1] = rng.integers(1, 4, n1); nd[n1 + n2:n1 + n2 + n3] = rng.integers(4, 6, n3)
            need = q[:, h[la]]; kk = back[need]
            at = np.argsort(np.argsort(np.where(need < TY, rng.random(need.shape), 2.0), axis=0), axis=0)
            kb = 2 * ((kk // 2 + 1 + rng.integers(0, 15, kk.shape)) % 16) + rng.integers(0, 2, kk.shape)
            new = np.where(at < nd, reg[o[b[kb] + (n[kb] * rng.random(kb.shape)).astype(np.int64)]], w[:, la])
            re_ = (np.arange(m) >= n1) & (np.arange(m) < n1 + n2)
            w[:, la] = np.where((at == 0) & re_, z[kk // 2], new)
            w0[r, g], x0[r, g], q0[r, g], s0[r, g], h0[r, g], v0[r, g] = w, x, q, s, h, v
    return pack(w0, x0, q0, s0, h0, v0, rng.choice(np.array([0, 1, 30, 60]), (N, 8, 16)))
def setup_inputs_full(rng):
    w = rng.integers(0, V, (N, 8, 16, V)); x = np.zeros((N, 8, 16, V), np.int64); q = np.full((N, 8, 16, TY), TY); s = rng.integers(0, 256, (N, 8, 16, TY))
    h = np.zeros((N, 8, V), np.int64); v = h.copy(); M = TY - 24; i = np.arange(V); edge = max(ST, LN) + LN; first = int(rng.integers(0, N))
    for a in range(N):
        r = (first + a) % N; role = a % 4; lo, hi = ((200, 241), (10, 41), (40, 121), (40, 121))[role]
        for g in range(8):
            ty = rng.permutation(TY); rest = ty[24:]
            b = rng.integers(lo, hi, (16, 1)); x[r, g] = b + rng.integers(-2, 3, (16, V))
            far = rng.integers(0, 21, (16, 8)); s[r, g][:, ty[:8]] = far if role == 0 else 255 - far
            s[r, g][:, ty[8:16]] = b + (2 * rng.integers(0, 2, (16, 8)) - 1) * rng.integers(5, 8, (16, 8)); s[r, g][:, ty[16:24]] = b
            sort = np.arange(M) % 4; at = np.argsort(rng.random((16, M)), axis=0)
            cnt = np.where(sort == 1, rng.integers(1, 4, M), np.where(sort == 2, rng.integers(1, 9, M), np.where(sort == 3, 1, 0)))
            pick = np.where(sort == 3, np.arange(M) // 4 % 8, rng.integers(0, 8, (16, M)))
            q[r, g][:, rest] = np.where(at < cnt, ty[8 * np.maximum(sort - 1, 0) + pick], TY)
            c = rng.integers(0, 4, V)
            if role == 0:
                c[:LN] = 1; v[r, g, LN:] = rng.random(V - LN) < 0.5
                if g % 4 == 3: c[:256] = 0
            elif role == 1: v[r, g] = rng.random(V) < 0.85
            elif role == 2: c = np.where(i < LN, 0, 2)
            else: c = np.where(i < edge, 1, 2); c[rng.permutation(LN)[:int(rng.integers(20, 29))]] = 0
            y = 4 * rng.integers(0, M // 4, V) + c
            if role == 2:
                o = np.arange(256, LN - 1, 4); goal = LN + rng.permutation(V - LN)[:len(o)]
                for k in (0, 1):
                    y[o + k] = 4 * (2 * rng.integers(0, M // 8, len(o)) + k) + 3
                    w[r, g, np.argmin(at[:, y[o + k]], axis=0), o + k] = goal
            h[r, g] = rest[y]
    for a in range(0, N - 1, 4):
        r, e = (first + a) % N, (first + a + 1) % N
        for g in (3, 7):
            k = np.arange(255 + SL, 255, -1); c = cand(np.add.reduce(WT[:, None] * x[r, g][:, k], axis=0) & (V - 1))
            top = np.max(x[e, g], axis=1) + 1; used = np.zeros(V, bool)
            for b in range(SL):
                if np.any(used[c[:, b]]): continue
                used[c[:, b]] = True; v[e, g, c[0, b]] = 1; v[e, g, c[15, b]] = 1
                x[e, g][:, c[0, b]] = top - (np.arange(16) == rng.integers(0, 16)); x[e, g][:, c[15, b]] = top
    return pack(w, x, q, s, h, v, 32 + rng.integers(0, 9, (N, 8, 16)))
def check_inputs(d):
    bad = []
    for k, lo, hi in (("wd", 0, V - 1), ("xs", 0, 255), ("rq", 0, TY), ("sg", 0, 255), ("hy", 0, TY - 1), ("vf", 0, 1), ("th", 0, 4080)):
        a = np.asarray(d[k]).astype(np.float64)
        if not (np.min(a) >= lo and np.max(a) <= hi): bad.append("range of " + k)
        elif np.any(a != np.floor(a)): bad.append("whole numbers of " + k)
    return bad
def reference(wd, xs, rq, sg, hy, vf, th):
    m = wd.astype(np.int64).reshape(N, 8, 16, V); x = xs.astype(np.float32).astype(np.int64).reshape(N, 8, 16, V)
    q = rq.astype(np.int64).reshape(N, 8, 16, TY); s = sg.astype(np.float32).astype(np.int64).reshape(N, 8, 16, TY)
    h = hy.astype(np.int64).reshape(N, 8, V); v = vf.reshape(N, 8, V) == 1; lim = th.astype(np.int64).reshape(N, 8, 16, 1)
    last = np.zeros(N, np.int64)
    for t in range(RO):
        d = 1 + t % (N - 1); order = (ST * t + np.arange(V)) % V
        m1, h1, v1 = m.copy(), h.copy(), v.copy(); now = np.zeros(N, np.int64)
        for r in range(N):
            e = (r + d) % N
            for g in range(8):
                a = order[~v[r, g][order]][:LN]
                w = m[r, g][:, a]; need = q[r, g][:, h[r, g][a]]
                other = (need < TY) & (h[r, g][w] != need)
                far = np.add.reduce(np.abs(x[r, g][:, w] - s[r, g][:, np.minimum(need, TY - 1)]), axis=0)
                fail = other & (far > lim[r, g] + (last[r] & 255))
                n = np.add.reduce(fail.astype(np.int64), axis=0); good = n == 0; much = n > 3
                now[r] += np.count_nonzero(good)
                v1[r, g, a[good]] = True
                y = h[r, g][a[much]]; h1[r, g, a[much]] = ((y * y >> 4) + 5 * y + n[much]) & (TY - 1)
                i = np.flatnonzero((n > 0) & (n < 4))[:SL]
                if len(i) > 0:
                    z = x[r, g][:, a[i]]; u = np.add.reduce(WT[:, None] * z, axis=0) & (V - 1); c = cand(u); k = np.arange(len(i))
                    gap = np.add.reduce(np.abs(x[e, g][:, c] - z[:, None, :]), axis=0)
                    gap = np.where(v[e, g][c], gap, 4096); b = np.argmin(gap, axis=0)
                    take = fail[:, i] & (gap[b, k] < 4096)
                    m1[r, g][:, a[i]] = np.where(take, m[e, g][:, c[b, k]], w[:, i])
                j = np.flatnonzero(good & np.any(other, axis=0))[:RT]
                if len(j) > 0:
                    p = np.argmax(other[:, j], axis=0); name, one = np.unique(w[p, j], return_index=True)
                    h1[r, g, name] = need[p, j][one]; v1[r, g, name] = False
        m, h, v, last = m1, h1, v1, now
    return {"ym": m.reshape(N, 128, V).astype(np.float32), "yh": h.astype(np.float32), "yv": v.astype(np.float32)}

@@ -1,0 +1,772 @@
+from concourse.mybir import AluOpType as A, AxisListType, ActivationFunctionType as F
+
+SCRATCH = {}
+SEMAPHORES = ["cV", "cS", "cP", "cG"]
+
+
+PLACE = {}
+_POOLED = ("BO", "LT", "EQ0", "GT", "ID", "TRI", "LPA", "LPB", "UW", "BOI", "BC", "ON", "D0", "D1", "X2D", "K34", "R1", "RD0", "RI",
+           "RC", "RH", "RX", "RD2", "R2", "RN", "RH12", "C1", "MK", "COLS", "CR", "MG", "MI", "BOf", "R1f", "R0f", "SW", "W8", "JW",
+           "J192", "DD", "LIM", "JC")
+
+
+def _buf(name, cols, dtype, where="sbuf"):
+    if name in _POOLED:
+        pool = "PB" if dtype == "bfloat16" else "PF"
+        at = SCRATCH[pool][1][1] if pool in SCRATCH else 0
+        PLACE[name] = (pool, at, cols, dtype)
+        SCRATCH[pool] = ("sbuf", [128, at + (cols + 15) // 16 * 16], dtype)
+    else:
+        PLACE[name] = (name, 0, cols, dtype)
+        SCRATCH[name] = (where, [128, cols], dtype)
+
+
+for _n, _c, _d in (
+        ("X", 2560, "bfloat16"), ("WD", 2560, "int32"), ("RQ", 1032, "int32"), ("SG", 1040, "bfloat16"),
+        ("TB", 2640, "bfloat16"), ("SXT", 2560, "bfloat16"), ("WU", 2048, "uint16"), ("WDE", 2560, "int32"),
+        ("YM", 2560, "float32"), ("hyb", 128, "int32"), ("vfb", 128, "int32"), ("x2b", 128, "bfloat16"),
+        ("thi", 1, "int32"), ("KI", 4, "int32"), ("COLS", 32, "float32"), ("CR", 256, "float32"), ("MG", 128, "float32"),
+        ("MI", 128, "float32"), ("BO", 128, "bfloat16"), ("BOf", 128, "float32"), ("LT", 128, "bfloat16"), ("EQ0", 128, "bfloat16"),
+        ("GT", 128, "bfloat16"), ("ID", 128, "bfloat16"), ("TRI", 128, "bfloat16"), ("LPA", 128, "bfloat16"), ("LPB", 128, "bfloat16"),
+        ("UW", 128, "bfloat16"), ("BOI", 128, "bfloat16"), ("BC", 128, "bfloat16"), ("ON", 128, "bfloat16"),
+        ("D0", 128, "bfloat16"), ("D1", 128, "bfloat16"), ("X2D", 128, "bfloat16"), ("K34", 128, "bfloat16"),
+        ("R1", 144, "bfloat16"), ("RD0", 144, "bfloat16"), ("RI", 144, "bfloat16"), ("RC", 144, "bfloat16"), ("RH", 144, "bfloat16"),
+        ("RX", 144, "bfloat16"), ("RD2", 144, "bfloat16"), ("R2", 144, "bfloat16"), ("RN", 144, "bfloat16"),
+        ("R1f", 144, "float32"), ("R0f", 144, "float32"), ("SW", 512, "float32"), ("RH12", 16, "bfloat16"),
+        ("W8", 24, "float32"), ("C1", 128, "bfloat16"), ("JI", 512, "float32"), ("JW", 32, "float32"), ("J192", 32, "float32"), ("DD", 64, "float32"),
+        ("LIM", 64, "float32"), ("JC", 64, "float32"), ("MK", 256, "bfloat16"), ("ZR", 512, "bfloat16"), ("ZF", 128, "float32"),
+        ("U0", 2064, "bfloat16"), ("UH", 2048, "bfloat16"), ("UL", 2048, "bfloat16"), ("UG", 2048, "bfloat16"),
+        ("NW", 128, "bfloat16"), ("CUM", 128, "float32"), ("POS", 128, "float32"), ("TTB", 384, "bfloat16"),
+        ("OF", 24, "float32"), ("OFu", 8, "uint16"), ("CW", 4352, "bfloat16"), ("CC", 512, "bfloat16"), ("CLu", 32, "uint16"),
+        ("OH", 512, "bfloat16"), ("EX", 64, "float32"), ("Li", 64, "int32"), ("Lu", 32, "uint16"), ("TBL", 512, "bfloat16"),
+        ("XL", 512, "bfloat16"), ("Wu", 512, "uint16"), ("Ku", 512, "uint16"), ("STu", 32, "uint16"), ("TY", 64, "int32"),
+        ("PM", 512, "bfloat16"), ("Kf", 512, "float32"), ("W4K", 512, "float32"), ("KX", 512, "float32"), ("UI", 512, "int32"),
+        ("P2", 512, "float32"), ("P1", 512, "float32"), ("OT", 512, "bfloat16"), ("FO", 512, "bfloat16"),
+        ("GA", 128, "bfloat16"), ("O0", 128, "bfloat16"),
+        ("sg0", 2048, "bfloat16"), ("sg1", 2048, "bfloat16"), ("mm0", 2048, "bfloat16"), ("mm1", 2048, "bfloat16"),
+        ("hg0", 2048, "bfloat16"), ("hg1", 2048, "bfloat16"),
+        ("LW", 416, "float32"), ("HLi", 192, "int32"), ("HLb", 64, "bfloat16"), ("RP", 64, "bfloat16"), ("GM", 32, "bfloat16"),
+        ("PFu", 32, "uint16"), ("P1W", 704, "float32"), ("P2W", 704, "float32"), ("TBn", 512, "bfloat16"), ("thB", 4, "float32"),
+        ("CN", 4, "int32"), ("AI", 512, "int32"), ("AF", 640, "float32"), ("AB", 704, "bfloat16"), ("AU", 8, "uint16"),
+        ("BI", 1200, "int32"), ("BF2", 560, "float32"), ("BU", 320, "uint16"), ("FL0", 128, "bfloat16"), ("FL1", 128, "bfloat16"),
+        ("FL2", 128, "bfloat16"), ("DW0", 136, "int32"), ("DW1", 136, "int32"), ("DW2", 136, "int32")):
+    _buf(_n, _c, _d)
+for _t in range(3):
+    _buf("XE%d" % _t, 2048, "bfloat16")
+    _buf("WE%d" % _t, 2048, "uint16")
+    _buf("FI%d" % _t, 128, "bfloat16")
+for _n in ("i01", "i02", "i12"):
+    _buf("D" + _n, 136, "int32")
+for _b in range(8):
+    _buf("q%d" % _b, 512, "float32", "psum")
+_NDMA, _NREM = 40, 12
+SEMAPHORES += ["d%d" % k for k in range(_NDMA)] + ["l%d" % k for k in range(_NREM)] + ["r%d" % k for k in range(_NREM)]
+
+
+def rank_program(g, core, T, topo):
+    rank = T.rank_of(core)
+    if rank is None:
+        return
+    N = len(T.cores)
+    eng = {"V": g.vector, "S": g.scalar, "P": g.tensor, "G": g, "Y": g.sync}
+    cnt = {"cV": 0, "cS": 0, "cP": 0, "cG": 0}
+    known = {e: {} for e in eng}
+    acc = {}
+    nd, sent, fin = [0], [], []
+    psum = {"q%d" % b for b in range(8)}
+
+    def v(name, lo=0, hi=None, step=1, rows=None):
+        buf, at, cols, _ = PLACE[name]
+        return (buf, at + lo, at + (cols if hi is None else hi), step, rows)
+
+    def ap(x):
+        name, lo, hi, step, rows = x
+        r = slice(None) if rows is None else rows
+        return T[name][r, lo:hi] if step == 1 else T[name][r, lo:hi:step]
+
+    def wait(e, sem, val, clock):
+        k = known[e]
+        if k.get(sem, 0) < val:
+            eng[e].wait_ge(T.sem[sem], val)
+            k[sem] = val
+        for s, c in clock.items():
+            if k.get(s, 0) < c:
+                k[s] = c
+
+    def deps(e, reads, writes):
+        need = []
+        for lst, wr in ((reads, False), (writes, True)):
+            for x in lst:
+                ex = x[0] in psum
+                for a in acc.get(x[0], ()):
+                    if ex and e == "P" and a[4] == "P":
+                        continue
+                    if ex and a[4] != e:
+                        need.append(a)
+                    elif a[1] < x[2] and x[1] < a[2] and (wr or a[3]) and (a[0] is None or x[4] is None or a[0] == x[4]):
+                        need.append(a)
+        need.sort(key=lambda a: -a[6])
+        for a in need:
+            wait(e, a[5], a[6], a[7])
+
+    def note(e, reads, writes, sem, val, clock):
+        for lst, wr in ((reads, False), (writes, True)):
+            for x in lst:
+                old = acc.setdefault(x[0], [])
+                if x[0] in psum:
+                    keep = [a for a in old if a[4] == e and not (wr and x[1] <= a[1] and a[2] <= x[2])]
+                elif wr and x[3] == 1:
+                    keep = [a for a in old if not (x[1] <= a[1] and a[2] <= x[2] and (x[4] is None or a[0] == x[4]))]
+                else:
+                    keep = [a for a in old if a[3] or a[4] != e or a[1:3] != (x[1], x[2]) or a[0] != x[4] or wr]
+                keep.append((x[4], x[1], x[2], wr, e, sem, val, clock))
+                acc[x[0]] = keep
+
+    prog = []
+
+    def call(e, emit, reads, writes, cost, lat=0.0):
+        prog.append({"e": e, "emit": emit, "r": reads, "w": writes, "cost": cost, "lat": lat})
+
+    def op(e, fn, reads, writes, cost=0.1):
+        def emit():
+            deps(e, reads, writes)
+            sem = "c" + e
+            cnt[sem] += 1
+            fn().then_inc(T.sem[sem], 1)
+            clock = dict(known[e])
+            clock[sem] = cnt[sem]
+            note(e, reads, writes, sem, cnt[sem], clock)
+        call(e, emit, reads, writes, cost)
+
+    def mms(*parts):
+        for n, lst in enumerate(parts):
+            first, last = n == 0, n == len(parts) - 1
+            cyc = sum(max(64, (r[2] - r[1]) // r[3]) * (4 if r[0] in ("AF", "BF2", "P2W") else 1) for _, _, r in lst)
+
+            def emit(lst=lst, first=first, last=last):
+                sem = "cP"
+                val = cnt[sem] + 1
+                for k, (o, l, r) in enumerate(lst):
+                    deps("P", [l, r], [o] if k == 0 else [])
+                    m = g.tensor.matmul(ap(o), ap(l), ap(r), first and k == 0, last and k == len(lst) - 1)
+                m.then_inc(T.sem[sem], 1)
+                cnt[sem] = val
+                clock = dict(known["P"])
+                clock[sem] = val
+                note("P", [x[1] for x in lst] + [x[2] for x in lst], [x[0] for x in lst], sem, val, clock)
+            call("P", emit, [x[1] for x in lst] + [x[2] for x in lst], [x[0] for x in lst], cyc * 0.52e-3)
+
+    def dma(e, out, in_, o=None, i=None):
+        sem = "d%d" % nd[0]
+        nd[0] += 1
+        rd, wr = ([] if in_ is None else [in_]), ([] if out is None else [out])
+
+        def emit():
+            deps(e, rd, wr)
+            eng[e].dma_start(ap(out) if o is None else o, ap(in_) if i is None else i).then_inc(T.sem[sem], 16)
+            clock = dict(known[e])
+            clock[sem] = 16
+            note("D" + sem, rd, wr, sem, 16, clock)
+        big = (out or in_)[4] is None and (out or in_)[2] - (out or in_)[1] > 512
+        call(e, emit, rd, wr, 0.06, 5.0 if big else 2.3)
+        return sem
+
+    def send(slot, to, out, in_):
+        dst = T.cores[to % N]
+        n = len(topo.engines(core, dst))
+        sent.append(("l%d" % slot, n))
+
+        def emit():
+            deps("G", [in_], [])
+            rid, pid, _ = topo.addr(dst)
+            g.remote_dma(ap(out), ap(in_), T.sem["r%d" % slot], T.sem["l%d" % slot], pid, rid, topo.mask(core, dst))
+            note("Dl%d" % slot, [in_], [], "l%d" % slot, n, {"l%d" % slot: n})
+        call("G", emit, [in_], [(slot, 0, 1, 1, None)], 1.2, 16.0 if slot < 6 else 4.0)
+
+    def arrive(slot, frm, buf):
+        n = len(topo.engines(T.cores[frm % N], core))
+        call("R", lambda: note("Dr%d" % slot, [], [buf], "r%d" % slot, n, {"r%d" % slot: n}), [(slot, 0, 1, 1, None)], [buf], 0.0)
+
+    def issue():
+        hist, pred = {}, []
+        for k, c in enumerate(prog):
+            ps = {}
+            for lst, wr in ((c["r"], False), (c["w"], True)):
+                for x in lst:
+                    h = hist.setdefault(x[0], [])
+                    for a in h:
+                        if a[0] == k:
+                            continue
+                        if x[0] in psum:
+                            hit = wr or a[4] or a[5] != c["e"]
+                        else:
+                            hit = (wr or a[4]) and a[1] < x[2] and x[1] < a[2] and (a[3] is None or x[4] is None or a[3] == x[4])
+                        if hit:
+                            ps[a[0]] = max(ps.get(a[0], 0.0), prog[a[0]]["lat"] + 0.1)
+            for lst, wr in ((c["r"], False), (c["w"], True)):
+                for x in lst:
+                    h = hist[x[0]]
+                    if wr and x[3] == 1:
+                        if x[0] in psum:
+                            h[:] = [a for a in h if a[0] == k]
+                        else:
+                            h[:] = [a for a in h if not (x[1] <= a[1] and a[2] <= x[2] and (x[4] is None or a[3] == x[4]))]
+                    e = (k, x[1], x[2], x[4], wr, c["e"])
+                    if e not in h:
+                        h.append(e)
+            pred.append(ps)
+        n = len(prog)
+        rank_, succ = [0.0] * n, [[] for _ in range(n)]
+        for k in range(n):
+            for p in pred[k]:
+                succ[p].append(k)
+        for k in range(n - 1, -1, -1):
+            rank_[k] = prog[k]["cost"] + max([rank_[s] + pred[s][k] for s in succ[k]] or [0.0])
+        left = [len(p) for p in pred]
+        at, free, done = [0.0] * n, {}, [0.0] * n
+        ready = {k for k in range(n) if left[k] == 0}
+        while ready:
+            best = None
+            for k in ready:
+                e = prog[k]["e"]
+                t0 = at[k] if e == "R" else max(at[k], free.get(e, 0.0))
+                key = (t0, -rank_[k], k)
+                if best is None or key < best:
+                    best = key
+            t0, _, k = best
+            ready.remove(k)
+            c = prog[k]
+            c["emit"]()
+            done[k] = t0 + c["cost"]
+            free[c["e"]] = done[k]
+            for s in succ[k]:
+                at[s] = max(at[s], done[k] + pred[s][k])
+                left[s] -= 1
+                if left[s] == 0:
+                    ready.add(s)
+
+    def wid(x):
+        return (x[2] - x[1] + x[3] - 1) // x[3]
+
+    def half(*xs):
+        return 0.5 if all(x[0] in two for x in xs) else 1.0
+
+    two = {p[0] for p in PLACE.values() if p[3] in ("bfloat16", "uint16")}
+
+    def ew(w, f=1.0):
+        return 0.03 + max(64, w * f) * 1.04e-3
+
+    def ind(win, off):
+        return ap(win).indirect(ap(off))
+
+    def tt(o, a, b, f):
+        k = 1 if a[0] in psum or b[0] in psum else 2 * half(o, a, b)
+        op("V", lambda: g.vector.tensor_tensor(ap(o), ap(a), ap(b), f), [a, b], [o], ew(wid(o), k))
+
+    def ts(o, a, s1, f, s2=None, f2=None):
+        rd = [a] + [x for x in (s1, s2) if isinstance(x, tuple)]
+        p1 = ap(s1) if isinstance(s1, tuple) else s1
+        p2 = ap(s2) if isinstance(s2, tuple) else s2
+        w = ew(wid(o), half(o, a))
+        if f2 is None:
+            op("V", lambda: g.vector.tensor_scalar(ap(o), ap(a), p1, None, f), rd, [o], w)
+        else:
+            op("V", lambda: g.vector.tensor_scalar(ap(o), ap(a), p1, p2, f, f2), rd, [o], w)
+
+    def cp(o, a):
+        op("V", lambda: g.vector.tensor_copy(ap(o), ap(a)), [a], [o], ew(wid(o), half(o, a)))
+
+    def ms(o, c):
+        op("V", lambda: g.vector.memset(ap(o), c), [], [o], ew(wid(o), half(o)))
+
+    def red(o, a):
+        op("V", lambda: g.vector.tensor_reduce(ap(o), ap(a), AxisListType.X, A.add), [a], [o], ew(wid(a)))
+
+    def asel(o, a, pattern, base):
+        op("G", lambda: g.affine_select(ap(o), ap(a), pattern, A.is_equal, 0.0, base, 1), [a], [o], 0.2 + 2.1e-3 * wid(o))
+
+    def gat(o, win, off):
+        op("V", lambda: g.vector.tensor_copy(ap(o), ind(win, off)), [win, off], [o], ew(wid(o), 1.5))
+
+    def sca(win, off, a):
+        op("V", lambda: g.vector.tensor_copy(ind(win, off), ap(a)), [a, off], [win], ew(wid(a), 3.5))
+
+    def gtt(o, win, off, b, f):
+        op("V", lambda: g.vector.tensor_tensor(ap(o), ind(win, off), ap(b), f), [win, off, b], [o], ew(wid(o), 1.6))
+
+    def scan(o, a, z, f):
+        w = ew(wid(o), half(o, a))
+        op("V", lambda: g.vector.tensor_tensor_scan(ap(o), ap(a), ap(z), 0.0, f, A.add), [a, z], [o], w)
+
+    def act(o, a, func=F.Copy, bias=None, scale=None):
+        kw = {}
+        rd = [a]
+        for k, x in (("bias", bias), ("scale", scale)):
+            if x is not None:
+                rd += [x]
+                kw[k] = ap(x)
+        op("S", lambda: g.scalar.activation(ap(o), ap(a), func, **kw), rd, [o], ew(wid(o)))
+
+    def sgat(o, win, off):
+        op("S", lambda: g.scalar.activation(ap(o), ind(win, off), F.Copy), [win, off], [o], ew(wid(o), 1.5))
+
+    def iota(o, pattern, base, ch=0):
+        if SCRATCH[o[0]][2] == "int32":
+            op("G", lambda: g.iota(ap(o), pattern, base, ch), [], [o], 0.2)
+        else:
+            op("G", lambda: g.iota(ap(o), pattern, base, ch, allow_small_or_imprecise_dtypes=True), [], [o], 0.2 + 2.1e-3 * wid(o))
+
+    def win(R, i):
+        return v(R, 15 - i, 143 - i)
+
+    dma("Y", v("vfb"), None, i=T.vf[:])
+    dma("S", v("hyb"), None, i=T.hy[:])
+    dma("Y", v("x2b"), None, i=T.xs[2:128:16, :])
+    dma("S", v("X", 0, 2048), None, i=T.xs[:])
+    dma("Y", v("WD", 0, 2048), None, i=T.wd[:])
+    dma("S", v("RQ", 0, 1024), None, i=T.rq[:])
+    dma("Y", v("SG", 0, 1024), None, i=T.sg[:])
+    dma("S", v("thi"), None, i=T.th[:])
+
+    iota(v("KI", 0, 1), [[1, 1]], 0, 1)
+    iota(v("CR"), [[1, 256]], 0)
+    iota(v("MG"), [[1, 8], [0, 16]], 0)
+    iota(v("MI"), [[0, 8], [1, 16]], 0)
+    iota(v("C1"), [[1, 128]], 0)
+    iota(v("JI"), [[1, 512]], 4097)
+    iota(v("JC", 0, 32), [[16, 32]], 0)
+    col = {}
+
+    def newcol(name):
+        k = len(col)
+        col[name] = v("COLS", k, k + 1)
+        return col[name]
+
+    ms(v("TB"), 0.0)
+    kif, kgf, kf = newcol("ki"), newcol("kg"), newcol("k")
+    ts(v("KI", 1, 2), v("KI", 0, 1), 4, A.arith_shift_right)
+    ts(v("KI", 2, 3), v("KI", 0, 1), 15, A.bitwise_and)
+    ts(v("KI", 3, 4), v("KI", 1, 2), 1, A.bitwise_and)
+    cp(kif, v("KI", 2, 3))
+    cp(kgf, v("KI", 1, 2))
+    cp(kf, v("KI", 0, 1))
+    odd, even = newcol("odd"), newcol("even")
+    cp(odd, v("KI", 3, 4))
+    ts(newcol("g15"), kgf, 16.0, A.mult, 15.0, A.add)
+    for q in range(5):
+        ts(newcol("q%d" % q), kif, float(q), A.is_equal)
+    ts(even, odd, 0.0, A.is_equal)
+    ts(newcol("c16"), col["q0"], 16.0, A.mult)
+    ts(newcol("c32"), col["q0"], 32.0, A.mult)
+    ts(newcol("x64"), col["q3"], -64.0, A.mult)
+    ts(newcol("b2"), col["q2"], 8192.0, A.mult)
+    ts(newcol("uw"), kif, 40960.0, A.mult, 4096.0, A.add)
+    ts(newcol("m2"), kif, 2.0, A.mult, 1.0, A.add)
+    ts(newcol("km"), kf, -16.0, A.add)
+    ts(newcol("kp"), kf, 16.0, A.add)
+    tt(newcol("h"), col["c32"], col["q1"], A.add)
+    tt(newcol("sx"), col["x64"], col["q4"], A.subtract)
+    tt(newcol("k34"), col["q3"], col["q4"], A.add)
+    ts(v("R1", 0, 143), v("CR", 0, 143), col["g15"], A.is_equal)
+    ts(v("BI", 0, 128), v("hyb"), 5, A.arith_shift_right)
+    ts(v("BI", 128, 256), v("hyb"), 31, A.bitwise_and)
+    ts(v("BF2", 0, 128), v("vfb"), -8192.0, A.mult, 8192.0, A.add)
+    tt(v("FL0"), v("BF2", 0, 128), v("x2b"), A.add)
+    dma("Y", v("TB", 0, 2048, 1, slice(2, 128, 16)), v("FL0"))
+    cp(v("AB", 0, 256), v("BI", 0, 256))
+    dma("Y", v("TB", 0, 2048, 1, slice(0, 128, 16)), v("AB", 0, 128))
+    dma("Y", v("TB", 0, 2048, 1, slice(1, 128, 16)), v("AB", 128, 256))
+    ts(v("BO"), v("MG"), kgf, A.is_equal)
+    ts(v("RD2", 0, 143), v("R1", 0, 143), col["q2"], A.mult)
+    ts(v("GT"), v("MI"), kif, A.is_lt)
+    ts(v("EQ0"), v("MI"), kif, A.is_equal)
+    ts(v("LT"), v("MI"), kif, A.is_gt)
+    tt(v("ID"), v("BO"), v("EQ0"), A.mult)
+    tt(v("GT"), v("GT"), v("BO"), A.mult)
+    ts(v("LPA"), v("ID"), 4096.0, A.mult)
+    tt(v("LPA"), v("LPA"), v("GT"), A.subtract)
+    ts(v("LPB"), v("ID"), -4096.0, A.mult)
+    tt(v("LPB"), v("LPB"), v("GT"), A.subtract)
+    ts(v("RH12", 0, 8), v("CR", 0, 8), kgf, A.is_gt)
+    ts(v("RH12", 8, 16), v("CR", 0, 8), kgf, A.is_equal)
+    ms(v("ZF"), 0.0)
+    ms(v("ZR"), 0.0)
+    ms(v("X", 2048, 2560), 0.0)
+    ms(v("WD", 2048, 2560), 0)
+    ms(v("RQ", 1024, 1032), 1024)
+    ms(v("SG", 1024, 1040), 0.0)
+    ms(v("CW", 0, 512), 0.0)
+    ts(v("TB", 2048, 2560), v("ZR"), col["c32"], A.add)
+    ts(v("JW"), v("JC", 0, 32), kif, A.add)
+    ts(v("W8", 0, 8), v("JW", 0, 8), 2048.0, A.add)
+    ts(v("W8", 8, 12), v("JW", 0, 4), 2560.0, A.add)
+    ts(v("JC", 32, 64), v("JW"), 2048.0, A.add)
+    for n_, c_ in (("RD0", "q0"), ("RI", "ki"), ("RC", "c16"), ("RH", "h"), ("RX", "sx"), ("R0f", "q0")):
+        act(v(n_, 0, 143), v("R1", 0, 143), scale=col[c_])
+    ms(v("SXT"), 0.0)
+    mms([(v("q7", 0, 128), win("R1", b), v("X", 128 * b, 128 * b + 128)) for b in range(16)])
+    cp(v("BI", 256, 384), v("q7", 0, 128))
+    ts(v("BI", 384, 512), v("BI", 256, 384), 6, A.arith_shift_right)
+    ts(v("BI", 512, 640), v("BI", 256, 384), 63, A.bitwise_and)
+    cp(v("AB", 256, 512), v("BI", 384, 640))
+    for q in (3, 4):
+        lo = 256 + 128 * (q - 3)
+        dma("Y", v("TB", 0, 2048, 1, slice(q, 128, 16)), v("AB", lo, lo + 128))
+        dma("Y", v("SXT", 0, 2048, 1, slice(q, 128, 16)), v("AB", lo, lo + 128))
+    send(0, rank - 1, v("XE0"), v("X", 0, 2048))
+    send(6, rank - 1, v("FI0"), v("FL0"))
+    arrive(6, rank + 1, v("FI0"))
+    cp(v("WU"), v("WD", 0, 2048))
+    send(3, rank - 1, v("WE0"), v("WU"))
+    for t in (1, 2):
+        send(t, rank - 1 - t, v("XE%d" % t), v("X", 0, 2048))
+        send(3 + t, rank - 1 - t, v("WE%d" % t), v("WU"))
+    for t in range(3):
+        arrive(t, rank + 1 + t, v("XE%d" % t))
+        arrive(3 + t, rank + 1 + t, v("WE%d" % t))
+
+    def late_constants():
+        ts(v("R2", 0, 143), v("R1", 0, 143), 2.0, A.mult)
+        ts(v("RN", 0, 143), v("R1", 0, 143), -1.0, A.mult)
+        act(v("R1f", 0, 143), v("R1", 0, 143))
+        act(v("BOf"), v("BO"))
+        for n_, c_ in (("UW", "uw"), ("BOI", "ki"), ("BC", "c16")):
+            act(v(n_), v("BO"), scale=col[c_])
+        for n_, c_ in (("D0", "q0"), ("D1", "q1"), ("X2D", "q2"), ("K34", "k34")):
+            act(v(n_), v("ID"), scale=col[c_])
+
+    def last_constants():
+        cp(v("thB", 0, 1), v("thi"))
+        cp(v("thB", 1, 2), v("thB", 0, 1))
+        tt(v("TRI"), v("BO"), v("LT"), A.mult)
+        ms(v("ON"), 1.0)
+        ts(v("J192"), v("JW"), 192.0, A.add)
+        ts(v("DD", 0, 32), v("JW"), 192.0 - 4095.0, A.add)
+        ts(v("DD", 32, 64), v("JW"), 64.0 - 4095.0, A.add)
+        ms(v("LIM", 0, 32), 128.0 - 4095.0)
+        ms(v("LIM", 32, 64), 64.0 - 4095.0)
+        for k, (c_, m_) in enumerate(((kf, even), (col["kp"], even), (col["km"], odd), (kf, odd))):
+            ts(v("SW", 128 * k, 128 * k + 128), v("CR", 0, 128), c_, A.is_equal, m_, A.mult)
+        for c in range(4):
+            ts(v("AF", 64 * c, 64 * c + 64), v("CR", 0, 64), -1.0, A.mult, 16.0 * c - 0.5, A.add)
+        ts(v("MK"), v("AF", 0, 256), kif, A.add, 0.0, A.is_gt)
+        ms(v("U0"), 0.0)
+        ms(v("U0", 0, 2064, 16), 1.0)
+        for q, n_ in enumerate(("UH", "UL", "UG")):
+            asel(v(n_), v("U0", 16 - q, 2064 - q), [[-1, 16], [-1, 128]], q)
+
+    def lanes(t):
+        c0 = 896 * t % 2048 // 16
+        mms([(v("q2", 0, 128), win("RD2", i), v("TB", i, 2048, 16)) for i in range(16)])
+        ts(v("NW", 0, 128 - c0), v("q2", c0, 128), 4096.0, A.is_ge)
+        if c0:
+            ts(v("NW", 128 - c0, 128), v("q2", 0, c0), 4096.0, A.is_ge)
+        mms([(v("q3", 0, 128), v("BO"), v("NW"))])
+        mms([(v("q4", 0, 128), v("NW"), v("BO"))])
+        mms([(v("q3", 128, 256), v("LPA"), v("NW"))])
+        act(v("TTB", 0, 128), v("q4", 0, 128))
+        scan(v("CUM"), v("q3", 0, 128), v("ZF"), A.add)
+        tt(v("TTB", 256, 384), v("q4", 0, 128), v("EQ0"), A.mult)
+        tt(v("TTB", 128, 256), v("q4", 0, 128), v("LT"), A.mult)
+        mms([(v("q5", 8, 16), v("TTB", 256, 384), v("RH12", 8, 16))])
+        mms([(v("q5", 0, 8), v("TTB", 0, 128), v("RH12", 0, 8)), (v("q5", 0, 8), v("TTB", 128, 256), v("RH12", 8, 16))])
+        tt(v("POS"), v("q3", 128, 256), v("CUM"), A.add)
+        ts(v("OF", 0, 8), v("q5", 8, 16), 0.5, A.is_lt)
+        tt(v("OF", 8, 16), v("OF", 0, 8), v("W8", 0, 8), A.mult)
+        tt(v("OF", 16, 24), v("q5", 0, 8), v("OF", 8, 16), A.add)
+        cp(v("OFu"), v("OF", 16, 24))
+        sca(v("CW"), v("OFu"), v("C1"))
+        ts(v("EX", 0, 32), v("JW"), v("CUM", 127, 128), A.is_ge)
+        tt(v("EX", 32, 64), v("EX", 0, 32), v("JC", 32, 64), A.mult)
+        scan(v("CC"), v("CW", 0, 512), v("ZR"), A.max)
+        mms([(v("q5", 32, 64), win("RD0", i), v("CC", i, 512, 16)) for i in range(16)])
+        cp(v("CLu"), v("q5", 32, 64))
+        gtt(v("OH"), v("POS"), v("CLu"), v("JI"), A.is_equal)
+        mms([(v("q6", 0, 32), win("RC", i), v("CC", i, 512, 16)) for i in range(16)],
+            [(v("q6", 0, 32), win("RI", i), v("OH", i, 512, 16)) for i in range(16)])
+        ts(v("Li", 0, 32), v("q6", 0, 32), float(16 * c0), A.add)
+        ts(v("Li", 32, 64), v("Li", 0, 32), 2047, A.bitwise_and)
+        tt(v("Li", 0, 32), v("Li", 32, 64), v("EX", 32, 64), A.max)
+        cp(v("Lu"), v("Li", 0, 32))
+
+    def fetch(t):
+        sgat(v("TBL"), v("TB"), v("Lu"))
+        gat(v("Wu"), v("WD"), v("Lu"))
+        mms([(v("q5", 64, 96), win("RH", i), v("TBL", i, 512, 16)) for i in range(16)])
+        cp(v("STu"), v("q5", 64, 96))
+        gat(v("Ku"), v("RQ"), v("STu"))
+
+    def check(t):
+        def ch(x, k):
+            return v(x, 128 * k, 128 * k + 128)
+
+        def sig(k):
+            sgat(v("sg%d" % (k & 1)), v("SG"), ch("Ku", k))
+
+        def typ(k, e):
+            (gat if e == "V" else sgat)(v("hg%d" % (k & 1)), v("TB"), ch("Wu", k))
+
+        def val(k):
+            gtt(v("mm%d" % (k & 1)), v("X"), ch("Wu", k), v("sg%d" % (k & 1)), A.max)
+
+        def sums(k):
+            q, h, s, m = "q%d" % (k & 1), "hg%d" % (k & 1), "sg%d" % (k & 1), "mm%d" % (k & 1)
+            mms([(v(q, 128, 256), win("RH", p), v(h, p, 2048, 16)) for p in range(16)])
+            mms([(v(q, 0, 128), win("RX", p), v(h, p, 2048, 16)) for p in range(16)],
+                [(v(q, 0, 128), win("RN", p), v(s, p, 2048, 16)) for p in range(16)],
+                [(v(q, 0, 128), win("R2", p), v(m, p, 2048, 16)) for p in range(16)])
+
+        def small(k):
+            q = "q%d" % (k & 1)
+            tt(v("O0"), v(q, 128, 256), ch("Kf", k), A.not_equal)
+            ts(v("GA"), v(q, 0, 128), v("thB", 1, 2), A.is_gt, 2.0, A.add)
+            tt(ch("OT", k), v("O0"), ch("PM", k), A.mult)
+            tt(ch("FO", k), ch("OT", k), v("GA"), A.mult)
+            tt(ch("P1", k), ch("W4K", k), ch("FO", k), A.add)
+
+        sig(0)
+        typ(0, "V")
+        val(0)
+        sums(0)
+        if t == 0:
+            last_constants()
+        sig(1)
+        typ(1, "S")
+        ts(v("PM"), v("Ku"), 1024.0, A.is_lt)
+        cp(v("Kf"), v("Ku"))
+        val(1)
+        sums(1)
+        sgat(v("XL"), v("X"), v("Lu"))
+        sig(2)
+        typ(2, "S")
+        ts(v("KX"), v("Ku"), 8192.0, A.mult)
+        ts(v("W4K"), v("Wu"), 4.0, A.mult)
+        tt(v("W4K"), v("W4K"), v("KX"), A.add)
+        small(0)
+        mms([(v("q6"), v("BC"), v("CC")), (v("q6"), v("BOI"), v("OH"))])
+        mms([(v("q7"), v("UW"), v("XL"))])
+        cp(v("UI"), v("q7"))
+        ts(v("UI"), v("UI"), 2047 << 12, A.bitwise_and)
+        tt(v("P2"), v("q6"), v("UI"), A.add)
+        val(2)
+        sums(2)
+        sig(3)
+        typ(3, "S")
+        small(1)
+        cp(v("TY", 0, 32), v("q5", 64, 96))
+        tt(v("HLi", 0, 32), v("TY", 0, 32), v("TY", 0, 32), A.mult)
+        ts(v("HLi", 0, 32), v("HLi", 0, 32), 4, A.arith_shift_right)
+        ts(v("HLi", 32, 64), v("TY", 0, 32), 5.0, A.mult)
+        tt(v("TY", 32, 64), v("HLi", 0, 32), v("HLi", 32, 64), A.add)
+        ms(v("P1W", 0, 192), 0.0)
+        ms(v("P2W", 0, 128), 2048.0)
+        ms(v("CW", 0, 512), 0.0)
+        val(3)
+        sums(3)
+        small(2)
+        small(3)
+
+    def post(t):
+        last = t == 2
+        c16 = 896 * t % 2048
+        lw = lambda k: v("LW", 32 * k, 32 * k + 32)
+        mms([(v("q3", 32, 64), win("R1", i), v("OT", i, 512, 16)) for i in range(16)])
+        mms([(v("q3", 0, 32), win("R1", i), v("FO", i, 512, 16)) for i in range(16)])
+        ts(lw(0), v("q3", 32, 64), -2.0, A.mult)
+        tt(lw(1), v("q3", 0, 32), lw(0), A.add)
+        ts(lw(4), lw(0), -1.0, A.is_lt)
+        ts(lw(2), lw(1), 0.5, A.is_lt)
+        ts(lw(3), lw(1), 3.5, A.is_lt)
+        tt(v("RP", 0, 32), lw(3), lw(2), A.subtract)
+        tt(v("RP", 32, 64), lw(4), lw(2), A.mult)
+        mms([(v("q4", 0, 64), v("BO"), v("RP"))])
+        mms([(v("q4", 64, 128), v("LPB"), v("RP"))])
+        mm = [(v("q6"), v("K34"), v("TBL")), (v("q6"), v("X2D"), v("XL"))]
+        tt(v("HLi", 64, 96), v("TY", 32, 64), lw(1), A.add)
+        scan(lw(5), v("q4", 0, 32), v("ZF", 0, 32), A.add)
+        scan(lw(6), v("q4", 32, 64), v("ZF", 0, 32), A.add)
+        ts(v("HLi", 64, 96), v("HLi", 64, 96), 1023, A.bitwise_and)
+        tt(v("LW", 224, 288), v("q4", 64, 128), v("LW", 160, 224), A.add)
+        ts(v("GM"), lw(2), -8192.0, A.mult)
+        tt(v("LW", 288, 352), v("LW", 224, 288), v("LIM"), A.is_lt)
+        tt(v("LW", 352, 416), v("LW", 224, 288), v("DD"), A.subtract)
+        tt(v("HLi", 64, 96), v("HLi", 64, 96), v("TY", 0, 32), A.subtract)
+        tt(v("LW", 352, 416), v("LW", 352, 416), v("LW", 288, 352), A.mult)
+        ts(lw(4), lw(3), 0.5, A.is_lt)
+        tt(lw(9), lw(11), lw(12), A.add)
+        tt(v("HLi", 64, 96), v("HLi", 64, 96), lw(4), A.mult)
+        tt(lw(9), lw(9), v("J192"), A.add)
+        tt(v("HLi", 64, 96), v("HLi", 64, 96), v("TY", 0, 32), A.add)
+        cp(v("PFu"), lw(9))
+        sca(v("P1W"), v("PFu"), v("P1"))
+        ts(v("HLi", 128, 160), v("HLi", 64, 96), 5, A.arith_shift_right)
+        ts(v("HLi", 160, 192), v("HLi", 64, 96), 31, A.bitwise_and)
+        cp(v("HLb"), v("HLi", 128, 192))
+        ai = lambda lo, hi: v("AI", lo, hi)
+        af = lambda lo, hi: v("AF", lo, hi)
+        ab = lambda lo, hi: v("AB", lo, hi)
+        cp(ai(0, 64), v("P1W", 128, 192))
+        ts(ai(64, 128), ai(0, 64), 2, A.bitwise_and)
+        ts(ab(0, 64), ai(64, 128), 0.5, A.mult)
+        mms([(v("q4", 0, 64), v("TRI"), ab(0, 64))])
+        sca(v("P2W"), v("PFu"), v("P2"))
+        for i in range(16):
+            for U, d in (("UH", v("HLb", 0, 32)), ("UL", v("HLb", 32, 64)), ("UG", v("GM"))):
+                mm.append((v("q6", i, 512, 16), v(U, 128 * i, 128 * i + 128), d))
+        ts(af(0, 64), v("q4", 0, 64), 0.5, A.is_lt)
+        tt(af(0, 64), af(0, 64), ab(0, 64), A.mult)
+        tt(af(64, 128), v("P1W", 128, 192), af(0, 64), A.mult)
+        mms([(v("q4", 64, 68), win("R1f", i), v("AF", 64 + i, 128, 16)) for i in range(16)])
+        mms([(v("q4", 0, 64), v("BOf"), af(64, 128))])
+        mms(mm[:2], mm[2:])
+        act(v("TBn"), v("q6"), F.Identity, bias=col["b2"])
+        bi = lambda k: v("BI", 128 * k, 128 * k + 128)
+        cp(bi(0), v("P2W", 0, 128))
+        cp(ai(128, 196), v("q4", 0, 68))
+        ts(bi(1), bi(0), 2047, A.bitwise_and)
+        ts(ai(196, 264), ai(128, 196), 2, A.arith_shift_right, 2047, A.bitwise_and)
+        if c16:
+            ts(bi(1), bi(1), float(c16), A.add)
+            ts(bi(1), bi(1), 2047, A.bitwise_and)
+        cp(af(128, 196), ai(196, 264))
+        cp(v("AU", 0, 4), ai(260, 264))
+        cp(v("BU", 0, 128), bi(1))
+        sgat(ab(320, 384), v("SXT"), v("AU", 0, 4))
+        sgat(v("sg0"), v("X"), v("BU", 0, 128))
+        ts(bi(2), bi(0), 12, A.arith_shift_right)
+        for c in range(4):
+            ts(ab(64 + 64 * c, 128 + 64 * c), af(128, 192), af(192 + c, 193 + c), A.is_equal)
+        tt(bi(3), bi(2), bi(2), A.mult)
+        ts(bi(4), bi(2), col["m2"], A.mult, kif, A.add)
+        tt(ab(64, 320), ab(64, 320), v("MK"), A.mult)
+        ts(bi(3), bi(3), 5, A.arith_shift_right)
+        for c in range(4):
+            red(af(200 + c, 201 + c), ab(64 + 64 * c, 128 + 64 * c))
+        tt(bi(3), bi(3), bi(4), A.add)
+        ts(ai(264, 268), ai(192, 196), 2, A.bitwise_and)
+        ts(bi(3), bi(3), 2047, A.bitwise_and)
+        ts(af(204, 208), af(200, 204), 0.5, A.is_gt)
+        ts(af(208, 212), ai(264, 268), 0.5, A.is_lt)
+        cp(v("BU", 128, 256), bi(3))
+        tt(af(204, 208), af(204, 208), af(208, 212), A.max)
+        ts(ai(272, 336), ai(128, 192), 18, A.arith_shift_right)
+        tt(af(204, 208), af(204, 208), v("W8", 8, 12), A.mult)
+        ts(ai(336, 400), ai(128, 192), 13, A.arith_shift_right, 31, A.bitwise_and)
+        tt(af(204, 208), af(204, 208), af(192, 196), A.max)
+        cp(ab(384, 512), ai(272, 400))
+        cp(v("AU", 4, 8), af(204, 208))
+        mms([(v("q2", 0, 64), v("ID"), ab(320, 384)), (v("q2", 0, 64), v("D0"), ab(384, 448)), (v("q2", 0, 64), v("D1"), ab(448, 512))])
+        act(ab(512, 576), v("q2", 0, 64), F.Identity, bias=col["b2"])
+        sca(v("TB"), v("Lu"), v("TBn"))
+        sca(v("TB"), v("AU", 4, 8), ab(512, 576))
+        if not last:
+            dma("Y", v("FL%d" % (t + 1)), v("TB", 0, 2048, 1, slice(2, 128, 16)))
+            send(7 + t, rank - 2 - t, v("FI%d" % (t + 1)), v("FL%d" % (t + 1)))
+            arrive(7 + t, rank + 2 + t, v("FI%d" % (t + 1)))
+            ts(v("EX", 0, 32), v("EX", 0, 32), 0.5, A.is_lt)
+            tt(v("EX", 0, 32), v("EX", 0, 32), lw(2), A.mult)
+            red(v("thB", 2, 3), v("EX", 0, 32))
+            cp(ab(576, 577), v("thB", 2, 3))
+
+    def bsum(t):
+        mms([(v("q3", 500, 501), v("ON"), v("AB", 576, 577))])
+        cp(v("CN", 0, 1), v("q3", 500, 501))
+        ts(v("CN", 1, 2), v("CN", 0, 1), 255, A.bitwise_and)
+        tt(v("thB", 1, 2), v("thB", 0, 1), v("CN", 1, 2), A.add)
+
+    def repairs(t):
+        bi = lambda k: v("BI", 128 * k, 128 * k + 128)
+        bf = lambda lo, hi: v("BF2", lo, hi)
+        sm = lambda k: v("BI", 1024 + 8 * k, 1032 + 8 * k)
+        xe, c16 = "XE%d" % t, 896 * t % 2048
+        mms([(v("q5", 0, 8), win("R0f", i), v("P2W", i, 128, 16)) for i in range(16)])
+        gtt(v("mm0"), v(xe), v("BU", 128, 256), v("sg0"), A.subtract)
+        act(v("hg0"), v("mm0"), F.Abs)
+        mms([(v("q7", 0, 128), win("R1", m), v("hg0", m, 2048, 16)) for m in range(16)])
+        cp(sm(0), v("q5", 0, 8))
+        cp(bi(4), v("P1W", 0, 128))
+        ts(sm(1), sm(0), 2047, A.bitwise_and)
+        ts(sm(2), sm(0), 12, A.arith_shift_right)
+        ts(bi(5), bi(4), 1, A.bitwise_and)
+        ts(bi(6), bi(4), 2, A.arith_shift_right, 2047, A.bitwise_and)
+        tt(sm(3), sm(2), sm(2), A.mult)
+        ts(sm(4), sm(2), 2.0, A.mult, 1.0, A.add)
+        if c16:
+            ts(sm(1), sm(1), float(c16), A.add)
+            ts(sm(1), sm(1), 2047, A.bitwise_and)
+        ts(sm(3), sm(3), 5, A.arith_shift_right)
+        ts(sm(5), sm(0), 2048, A.bitwise_and)
+        tt(sm(3), sm(3), sm(2), A.add)
+        ts(bf(520, 528), sm(5), 0.5, A.is_gt)
+        ts(bf(0, 128), v("q7", 0, 128), 16.0, A.mult, kif, A.add)
+        op("V", lambda: g.vector.transpose(ap(bf(128, 256)), ap(bf(0, 128))), [bf(0, 128)], [bf(128, 256)])
+        lo, n, o = 128, 128, 256
+        while n > 8:
+            tt(bf(o, o + n // 2), v("BF2", lo, lo + n, 2), v("BF2", lo + 1, lo + n, 2), A.min)
+            lo, n, o = o, n // 2, o + n // 2
+        for s1 in (0, 1):
+            mms([(v("q7", 256 + s1, 264, 2), v("SW", 256 * s1 + 128 * g2, 256 * s1 + 128 * g2 + 128), v("BF2", lo + g2, lo + 8, 2)) for g2 in (0, 1)])
+        cp(sm(6), v("q7", 256, 264))
+        ts(bf(528, 536), v("q7", 256, 264), 65400.0, A.is_gt)
+        ts(sm(7), sm(6), 15, A.bitwise_and)
+        tt(bf(528, 536), bf(528, 536), bf(520, 528), A.max)
+        tt(sm(7), sm(7), sm(4), A.mult)
+        tt(bf(528, 536), bf(528, 536), v("W8", 0, 8), A.mult)
+        tt(sm(7), sm(7), sm(3), A.add)
+        dw = "DW%d" % t
+        tt(v(dw, 128, 136), bf(528, 536), sm(1), A.max)
+        ts(sm(7), sm(7), 2047, A.bitwise_and)
+        cp(v("BU", 264, 272), v(dw, 128, 136))
+        cp(v("BU", 256, 264), sm(7))
+        gat(bi(7), v("WDE"), v("BU", 256, 264))
+        tt(bi(7), bi(7), bi(6), A.subtract)
+        tt(bi(7), bi(7), bi(5), A.mult)
+        tt(v(dw, 0, 128), bi(7), bi(6), A.add)
+        if t == 2:
+            cp(v("BF2", 0, 128), v(dw, 0, 128))
+            sca(v("YM"), v("BU", 264, 272), v("BF2", 0, 128))
+            fin.append(dma("Y", None, v("YM", 0, 2048), o=T.ym[:]))
+            return
+        sca(v("WD"), v("BU", 264, 272), v(dw, 0, 128))
+        for t2 in range(t + 1, 3):
+            slot = 9 + t + t2 - 1
+            send(slot, rank - 1 - t2, v("Di%d%d" % (t, t2)), v(dw))
+            arrive(slot, rank + 1 + t2, v("Di%d%d" % (t, t2)))
+
+    def helper(t):
+        dma("Y", v("XE%d" % t, 0, 2048, 1, slice(2, 128, 16)), v("FI%d" % t))
+        cp(v("WDE", 0, 2048), v("WE%d" % t))
+        for s in range(t):
+            b = "Di%d%d" % (s, t)
+            cp(v("BU", 272, 280), v(b, 128, 136))
+            sca(v("WDE"), v("BU", 272, 280), v(b, 0, 128))
+
+    def flags_out():
+        mms([(v("q2", 0, 128), win("RH", b), v("TB", 128 * b, 128 * b + 128)) for b in range(16)])
+        mms([(v("q2", 128, 256), win("RD2", b), v("TB", 128 * b, 128 * b + 128)) for b in range(16)])
+        cp(v("CUM"), v("q2", 0, 128))
+        ts(v("POS"), v("q2", 128, 256), 4096.0, A.is_lt)
+        fin.append(dma("Y", None, v("CUM"), o=T.yh[:]))
+        fin.append(dma("Y", None, v("POS"), o=T.yv[:]))
+
+    late_constants()
+    for t in range(3):
+        lanes(t)
+        fetch(t)
+        check(t)
+        helper(t)
+        if t == 2:
+            cp(v("YM"), v("WD"))
+        post(t)
+        if t == 2:
+            flags_out()
+        repairs(t)
+        if t < 2:
+            bsum(t)
+    issue()
+    for sem in fin:
+        wait("Y", sem, 16, {})
+    for sem, n in sent:
+        wait("G", sem, n, {})
+    for sem in cnt:
+        wait("G", sem, cnt[sem], {})

@@ -1,5 +1,6 @@
 from concourse.mybir import AluOpType as A, AxisListType, ActivationFunctionType as F
 
+PATIENCE = 0.5
 SCRATCH = {}
 SEMAPHORES = ["cV", "cS", "cP", "cG"]
 
@@ -7,7 +8,7 @@ SEMAPHORES = ["cV", "cS", "cP", "cG"]
 PLACE = {}
 _POOLED = ("BO", "LT", "EQ0", "GT", "ID", "TRI", "LPA", "LPB", "UW", "BOI", "BC", "ON", "D0", "D1", "X2D", "K34", "R1", "RD0", "RI",
            "RC", "RH", "RX", "RD2", "R2", "RN", "RH12", "C1", "MK", "COLS", "CR", "MG", "MI", "BOf", "R1f", "R0f", "SW", "W8", "JW",
-           "J192", "DD", "LIM", "JC")
+           "J192", "DD", "LIM", "JC", "NI", "RU", "RH8", "UD")
 
 
 def _buf(name, cols, dtype, where="sbuf"):
@@ -22,9 +23,10 @@ def _buf(name, cols, dtype, where="sbuf"):
 
 
 for _n, _c, _d in (
-        ("X", 2560, "bfloat16"), ("WD", 2560, "int32"), ("RQ", 1032, "int32"), ("SG", 1040, "bfloat16"),
-        ("TB", 2640, "bfloat16"), ("SXT", 2560, "bfloat16"), ("WU", 2048, "uint16"), ("WDE", 2560, "int32"),
-        ("YM", 2560, "float32"), ("hyb", 128, "int32"), ("vfb", 128, "int32"), ("x2b", 128, "bfloat16"),
+        ("X", 2560, "bfloat16"), ("WD", 2560, "float32"), ("RQ", 1032, "float32"), ("SG", 1040, "bfloat16"),
+        ("TB", 2640, "bfloat16"), ("SXT", 2048, "bfloat16"), ("WI", 2048, "int32"), ("RI32", 1024, "int32"), ("NI", 128, "bfloat16"),
+        ("FOf", 512, "float32"), ("RU", 144, "bfloat16"), ("UD", 128, "bfloat16"),
+        ("hyb", 128, "int32"), ("vfb", 128, "int32"), ("x2b", 128, "bfloat16"),
         ("thi", 1, "int32"), ("KI", 4, "int32"), ("COLS", 32, "float32"), ("CR", 256, "float32"), ("MG", 128, "float32"),
         ("MI", 128, "float32"), ("BO", 128, "bfloat16"), ("BOf", 128, "float32"), ("LT", 128, "bfloat16"), ("EQ0", 128, "bfloat16"),
         ("GT", 128, "bfloat16"), ("ID", 128, "bfloat16"), ("TRI", 128, "bfloat16"), ("LPA", 128, "bfloat16"), ("LPB", 128, "bfloat16"),
@@ -39,35 +41,68 @@ for _n, _c, _d in (
         ("NW", 128, "bfloat16"), ("CUM", 128, "float32"), ("POS", 128, "float32"), ("TTB", 384, "bfloat16"),
         ("OF", 24, "float32"), ("OFu", 8, "uint16"), ("CW", 4352, "bfloat16"), ("CC", 512, "bfloat16"), ("CLu", 32, "uint16"),
         ("OH", 512, "bfloat16"), ("EX", 64, "float32"), ("Li", 64, "int32"), ("Lu", 32, "uint16"), ("TBL", 512, "bfloat16"),
-        ("XL", 512, "bfloat16"), ("Wu", 512, "uint16"), ("Ku", 512, "uint16"), ("STu", 32, "uint16"), ("TY", 64, "int32"),
-        ("PM", 512, "bfloat16"), ("Kf", 512, "float32"), ("W4K", 512, "float32"), ("KX", 512, "float32"), ("UI", 512, "int32"),
-        ("P2", 512, "float32"), ("P1", 512, "float32"), ("OT", 512, "bfloat16"), ("FO", 512, "bfloat16"),
-        ("GA", 128, "bfloat16"), ("O0", 128, "bfloat16"),
-        ("sg0", 2048, "bfloat16"), ("sg1", 2048, "bfloat16"), ("mm0", 2048, "bfloat16"), ("mm1", 2048, "bfloat16"),
-        ("hg0", 2048, "bfloat16"), ("hg1", 2048, "bfloat16"),
+        ("Wu", 512, "uint16"), ("Ku", 512, "uint16"), ("STu", 32, "uint16"), ("TY", 64, "int32"),
+        ("PM", 512, "bfloat16"), ("W4", 512, "float32"), ("W4K", 512, "float32"), ("KX", 512, "float32"),
+        ("P2", 512, "float32"), ("FT", 1024, "bfloat16"),
+        ("ED", 320, "int32"), ("GA", 160, "bfloat16"), ("O0", 160, "bfloat16"),
+        ("sg0", 2560, "bfloat16"), ("sg1", 2560, "bfloat16"), ("mm0", 2560, "bfloat16"), ("mm1", 2560, "bfloat16"),
+        ("hg0", 2560, "bfloat16"), ("hg1", 2560, "bfloat16"),
         ("LW", 416, "float32"), ("HLi", 192, "int32"), ("HLb", 64, "bfloat16"), ("RP", 64, "bfloat16"), ("GM", 32, "bfloat16"),
         ("PFu", 32, "uint16"), ("P1W", 704, "float32"), ("P2W", 704, "float32"), ("TBn", 512, "bfloat16"), ("thB", 4, "float32"),
         ("CN", 4, "int32"), ("AI", 512, "int32"), ("AF", 640, "float32"), ("AB", 704, "bfloat16"), ("AU", 8, "uint16"),
         ("BI", 1200, "int32"), ("BF2", 560, "float32"), ("BU", 320, "uint16"), ("FL0", 128, "bfloat16"), ("FL1", 128, "bfloat16"),
-        ("FL2", 128, "bfloat16"), ("DW0", 136, "int32"), ("DW1", 136, "int32"), ("DW2", 136, "int32")):
+        ("FL2", 128, "bfloat16"), ("DW0", 136, "float32"), ("DW1", 136, "float32"), ("DW2", 136, "float32")):
     _buf(_n, _c, _d)
 for _t in range(3):
     _buf("XE%d" % _t, 2048, "bfloat16")
-    _buf("WE%d" % _t, 2048, "uint16")
+    _buf("WE%d" % _t, 2176, "float32")
     _buf("FI%d" % _t, 128, "bfloat16")
 for _n in ("i01", "i02", "i12"):
-    _buf("D" + _n, 136, "int32")
+    _buf("D" + _n, 136, "float32")
 for _b in range(8):
     _buf("q%d" % _b, 512, "float32", "psum")
-_NDMA, _NREM = 40, 12
+_NDMA, _NREM = 40, 15
 SEMAPHORES += ["d%d" % k for k in range(_NDMA)] + ["l%d" % k for k in range(_NREM)] + ["r%d" % k for k in range(_NREM)]
+
+
+def relay_of(core, T, topo):
+    return [c for c in topo.cores_of(core) if T.rank_of(c) is None and topo.die(c) != topo.die(core)
+            and all(topo.may_write(c, d) for d in T.cores)][0]
+
+
+def lanes_of(src, dst, T, topo):
+    far = [d for d in T.cores if topo.chip(d) != topo.chip(src)][0]
+    e = [k for k in topo.engines(src, dst) if k in topo.engines(src, far)]
+    return sum(1 << k for k in e), len(e)
+
+
+def relay_program(g, core, T, topo):
+    own = [c for c in T.cores if topo.chip(c) == topo.chip(core)]
+    if not own or relay_of(own[0], T, topo) != core:
+        return
+    rank, sent = T.rank_of(own[0]), []
+    n_on = lanes_of(own[0], core, T, topo)[1]
+    for slot, d, name, lo, hi, src in ((14, 1, "WE0", 1024, 2048, "WD"), (1, 2, "XE1", 0, 2048, "X"), (4, 2, "WE1", 0, 2048, "WD"), (2, 3, "XE2", 0, 2048, "X")):
+        if slot == 14:
+            g.wait_ge(T.sem.r13, n_on)
+        if slot == 1:
+            g.wait_ge(T.sem.r12, n_on)
+        dst = T.cores[(rank - d) % len(T.cores)]
+        mask, n = lanes_of(core, dst, T, topo)
+        rid, pid, _ = topo.addr(dst)
+        g.remote_dma(T[name][:, lo:hi], T[src][:, lo:hi], T.sem["r%d" % slot], T.sem["l%d" % slot], pid, rid, mask)
+        sent.append((slot, n))
+    for slot, n in sent:
+        g.wait_ge(T.sem["l%d" % slot], n)
 
 
 def rank_program(g, core, T, topo):
     rank = T.rank_of(core)
     if rank is None:
+        relay_program(g, core, T, topo)
         return
     N = len(T.cores)
+    GQ = ("gq", 0, 1, 1, None)
     eng = {"V": g.vector, "S": g.scalar, "P": g.tensor, "G": g, "Y": g.sync}
     cnt = {"cV": 0, "cS": 0, "cP": 0, "cG": 0}
     known = {e: {} for e in eng}
@@ -154,7 +189,7 @@ def rank_program(g, core, T, topo):
                 clock = dict(known["P"])
                 clock[sem] = val
                 note("P", [x[1] for x in lst] + [x[2] for x in lst], [x[0] for x in lst], sem, val, clock)
-            call("P", emit, [x[1] for x in lst] + [x[2] for x in lst], [x[0] for x in lst], cyc * 0.52e-3)
+            call("P", emit, [x[1] for x in lst] + [x[2] for x in lst], [x[0] for x in lst], cyc * 0.7e-3)
 
     def dma(e, out, in_, o=None, i=None):
         sem = "d%d" % nd[0]
@@ -172,20 +207,20 @@ def rank_program(g, core, T, topo):
         return sem
 
     def send(slot, to, out, in_):
-        dst = T.cores[to % N]
-        n = len(topo.engines(core, dst))
+        dst = relay_of(core, T, topo) if to is None else T.cores[to % N]
+        mask, n = lanes_of(core, dst, T, topo)
         sent.append(("l%d" % slot, n))
 
         def emit():
             deps("G", [in_], [])
             rid, pid, _ = topo.addr(dst)
-            g.remote_dma(ap(out), ap(in_), T.sem["r%d" % slot], T.sem["l%d" % slot], pid, rid, topo.mask(core, dst))
+            g.remote_dma(ap(out), ap(in_), T.sem["r%d" % slot], T.sem["l%d" % slot], pid, rid, mask)
             note("Dl%d" % slot, [in_], [], "l%d" % slot, n, {"l%d" % slot: n})
-        call("G", emit, [in_], [(slot, 0, 1, 1, None)], 1.2, 16.0 if slot < 6 else 4.0)
+        call("G", emit, [in_], [(slot, 0, 1, 1, None), GQ], 1.2, 0.0)
 
-    def arrive(slot, frm, buf):
-        n = len(topo.engines(T.cores[frm % N], core))
-        call("R", lambda: note("Dr%d" % slot, [], [buf], "r%d" % slot, n, {"r%d" % slot: n}), [(slot, 0, 1, 1, None)], [buf], 0.0)
+    def arrive(slot, buf, left, way):
+        n = lanes_of(T.cores[(rank + 1) % N], core, T, topo)[1]
+        call("R", lambda: note("Dr%d" % slot, [], [buf], "r%d" % slot, n, {"r%d" % slot: n}), [(left, 0, 1, 1, None)], [buf], way)
 
     def issue():
         hist, pred = {}, []
@@ -202,7 +237,7 @@ def rank_program(g, core, T, topo):
                         else:
                             hit = (wr or a[4]) and a[1] < x[2] and x[1] < a[2] and (a[3] is None or x[4] is None or a[3] == x[4])
                         if hit:
-                            ps[a[0]] = max(ps.get(a[0], 0.0), prog[a[0]]["lat"] + 0.1)
+                            ps[a[0]] = max(ps.get(a[0], 0.0), 0.0 if x == GQ else prog[a[0]]["lat"] + 0.1)
             for lst, wr in ((c["r"], False), (c["w"], True)):
                 for x in lst:
                     h = hist[x[0]]
@@ -234,6 +269,12 @@ def rank_program(g, core, T, topo):
                 if best is None or key < best:
                     best = key
             t0, _, k = best
+            e, late = prog[k]["e"], t0 + PATIENCE * prog[k]["cost"]
+            if e in ("V", "S", "P"):
+                for j in ready:
+                    if prog[j]["e"] == e and at[j] < late and (rank_[j], -j) > (rank_[k], -k):
+                        k = j
+                t0 = max(at[k], free.get(e, 0.0))
             ready.remove(k)
             c = prog[k]
             c["emit"]()
@@ -283,7 +324,7 @@ def rank_program(g, core, T, topo):
         op("V", lambda: g.vector.tensor_reduce(ap(o), ap(a), AxisListType.X, A.add), [a], [o], ew(wid(a)))
 
     def asel(o, a, pattern, base):
-        op("G", lambda: g.affine_select(ap(o), ap(a), pattern, A.is_equal, 0.0, base, 1), [a], [o], 0.2 + 2.1e-3 * wid(o))
+        op("G", lambda: g.affine_select(ap(o), ap(a), pattern, A.is_equal, 0.0, base, 1), [a], [o, GQ], 0.2 + 2.1e-3 * wid(o))
 
     def gat(o, win, off):
         op("V", lambda: g.vector.tensor_copy(ap(o), ind(win, off)), [win, off], [o], ew(wid(o), 1.5))
@@ -298,17 +339,21 @@ def rank_program(g, core, T, topo):
         w = ew(wid(o), half(o, a))
         op("V", lambda: g.vector.tensor_tensor_scan(ap(o), ap(a), ap(z), 0.0, f, A.add), [a, z], [o], w)
 
-    def act(o, a, func=F.Copy, bias=None, scale=None):
+    def act(o, a, func=F.Copy, bias=None, scale=None, accum_out=None):
         kw = {}
         rd = [a]
         for k, x in (("bias", bias), ("scale", scale)):
-            if x is not None:
+            if isinstance(x, tuple):
                 rd += [x]
                 kw[k] = ap(x)
-        op("S", lambda: g.scalar.activation(ap(o), ap(a), func, **kw), rd, [o], ew(wid(o)))
+            elif x is not None:
+                kw[k] = x
+        if accum_out is not None:
+            kw["accum_out"] = ap(accum_out)
+        op("S", lambda: g.scalar.activation(ap(o), ap(a), func, **kw), rd, [o] + ([] if accum_out is None else [accum_out]), ew(wid(o)))
 
-    def sgat(o, win, off):
-        op("S", lambda: g.scalar.activation(ap(o), ind(win, off), F.Copy), [win, off], [o], ew(wid(o), 1.5))
+    def sgat(o, win, off, scale=1.0):
+        op("S", lambda: g.scalar.activation(ap(o), ind(win, off), F.Copy, scale=scale), [win, off], [o], ew(wid(o), 1.5))
 
     def iota(o, pattern, base, ch=0):
         if SCRATCH[o[0]][2] == "int32":
@@ -323,8 +368,8 @@ def rank_program(g, core, T, topo):
     dma("S", v("hyb"), None, i=T.hy[:])
     dma("Y", v("x2b"), None, i=T.xs[2:128:16, :])
     dma("S", v("X", 0, 2048), None, i=T.xs[:])
-    dma("Y", v("WD", 0, 2048), None, i=T.wd[:])
-    dma("S", v("RQ", 0, 1024), None, i=T.rq[:])
+    dma("Y", v("WI"), None, i=T.wd[:])
+    dma("S", v("RI32"), None, i=T.rq[:])
     dma("Y", v("SG", 0, 1024), None, i=T.sg[:])
     dma("S", v("thi"), None, i=T.th[:])
 
@@ -353,20 +398,26 @@ def rank_program(g, core, T, topo):
     odd, even = newcol("odd"), newcol("even")
     cp(odd, v("KI", 3, 4))
     ts(newcol("g15"), kgf, 16.0, A.mult, 15.0, A.add)
-    for q in range(5):
+    for q in range(8):
         ts(newcol("q%d" % q), kif, float(q), A.is_equal)
     ts(even, odd, 0.0, A.is_equal)
     ts(newcol("c16"), col["q0"], 16.0, A.mult)
     ts(newcol("c32"), col["q0"], 32.0, A.mult)
     ts(newcol("x64"), col["q3"], -64.0, A.mult)
     ts(newcol("b2"), col["q2"], 8192.0, A.mult)
-    ts(newcol("uw"), kif, 40960.0, A.mult, 4096.0, A.add)
+    ts(newcol("uw"), kif, 10.0, A.mult, 1.0, A.add)
+    ts(newcol("u32"), col["q5"], 32.0 * 4096.0, A.mult)
+    ts(newcol("u1"), col["q6"], 4096.0, A.mult)
+    tt(newcol("ud"), col["u32"], col["u1"], A.add)
     ts(newcol("m2"), kif, 2.0, A.mult, 1.0, A.add)
     ts(newcol("km"), kf, -16.0, A.add)
     ts(newcol("kp"), kf, 16.0, A.add)
+    ts(newcol("k5"), kf, -5.0, A.add)
     tt(newcol("h"), col["c32"], col["q1"], A.add)
-    tt(newcol("sx"), col["x64"], col["q4"], A.subtract)
-    tt(newcol("k34"), col["q3"], col["q4"], A.add)
+    ts(newcol("keep"), kif, 2.5, A.is_gt)
+    ts(newcol("sx"), col["h"], 8192.0, A.mult)
+    tt(col["sx"], col["sx"], col["x64"], A.add)
+    tt(col["sx"], col["sx"], col["q4"], A.subtract)
     ts(v("R1", 0, 143), v("CR", 0, 143), col["g15"], A.is_equal)
     ts(v("BI", 0, 128), v("hyb"), 5, A.arith_shift_right)
     ts(v("BI", 128, 256), v("hyb"), 31, A.bitwise_and)
@@ -392,8 +443,10 @@ def rank_program(g, core, T, topo):
     ms(v("ZF"), 0.0)
     ms(v("ZR"), 0.0)
     ms(v("X", 2048, 2560), 0.0)
-    ms(v("WD", 2048, 2560), 0)
-    ms(v("RQ", 1024, 1032), 1024)
+    ms(v("WD", 2048, 2560), 0.0)
+    for t in range(3):
+        ms(v("WE%d" % t, 2048, 2176), 0.0)
+    ms(v("RQ", 1024, 1032), 1024.0)
     ms(v("SG", 1024, 1040), 0.0)
     ms(v("CW", 0, 512), 0.0)
     ts(v("TB", 2048, 2560), v("ZR"), col["c32"], A.add)
@@ -401,39 +454,49 @@ def rank_program(g, core, T, topo):
     ts(v("W8", 0, 8), v("JW", 0, 8), 2048.0, A.add)
     ts(v("W8", 8, 12), v("JW", 0, 4), 2560.0, A.add)
     ts(v("JC", 32, 64), v("JW"), 2048.0, A.add)
-    for n_, c_ in (("RD0", "q0"), ("RI", "ki"), ("RC", "c16"), ("RH", "h"), ("RX", "sx"), ("R0f", "q0")):
+    for n_, c_ in (("RD0", "q0"), ("RI", "ki"), ("RC", "c16"), ("RH", "h"), ("RX", "sx"), ("R0f", "q0"), ("RU", "uw")):
         act(v(n_, 0, 143), v("R1", 0, 143), scale=col[c_])
-    ms(v("SXT"), 0.0)
+    dma("Y", v("TB", 0, 2048, 1, slice(7, 128, 16)), v("x2b"))
     mms([(v("q7", 0, 128), win("R1", b), v("X", 128 * b, 128 * b + 128)) for b in range(16)])
-    cp(v("BI", 256, 384), v("q7", 0, 128))
-    ts(v("BI", 384, 512), v("BI", 256, 384), 6, A.arith_shift_right)
-    ts(v("BI", 512, 640), v("BI", 256, 384), 63, A.bitwise_and)
-    cp(v("AB", 256, 512), v("BI", 384, 640))
-    for q in (3, 4):
-        lo = 256 + 128 * (q - 3)
-        dma("Y", v("TB", 0, 2048, 1, slice(q, 128, 16)), v("AB", lo, lo + 128))
-        dma("Y", v("SXT", 0, 2048, 1, slice(q, 128, 16)), v("AB", lo, lo + 128))
-    send(0, rank - 1, v("XE0"), v("X", 0, 2048))
+    mms([(v("q7", 128, 256), win("RU", b), v("X", 128 * b, 128 * b + 128)) for b in range(16)])
+    cp(v("BI", 256, 512), v("q7", 0, 256))
+    ts(v("BI", 512, 640), v("BI", 256, 384), 6, A.arith_shift_right)
+    ts(v("BI", 640, 768), v("BI", 256, 384), 63, A.bitwise_and)
+    ts(v("BI", 768, 896), v("BI", 384, 512), 5, A.arith_shift_right, 63, A.bitwise_and)
+    ts(v("BI", 896, 1024), v("BI", 384, 512), 31, A.bitwise_and)
+    cp(v("CW", 512, 1024), v("BI", 512, 1024))
+    for q in range(3, 7):
+        dma("Y", v("TB", 0, 2048, 1, slice(q, 128, 16)), v("CW", 128 * q + 128, 128 * q + 256))
+    cp(v("SXT"), v("TB", 0, 2048))
+    cp(v("RQ", 0, 1024), v("RI32"))
+    cp(v("WD", 0, 2048), v("WI"))
     send(6, rank - 1, v("FI0"), v("FL0"))
-    arrive(6, rank + 1, v("FI0"))
-    cp(v("WU"), v("WD", 0, 2048))
-    send(3, rank - 1, v("WE0"), v("WU"))
-    for t in (1, 2):
-        send(t, rank - 1 - t, v("XE%d" % t), v("X", 0, 2048))
-        send(3 + t, rank - 1 - t, v("WE%d" % t), v("WU"))
-    for t in range(3):
-        arrive(t, rank + 1 + t, v("XE%d" % t))
-        arrive(3 + t, rank + 1 + t, v("WE%d" % t))
+    send(0, rank - 1, v("XE0"), v("X", 0, 2048))
+    send(13, None, v("WD", 0, 2048), v("WD", 0, 2048))
+    send(3, rank - 1, v("WE0", 0, 1024), v("WD", 0, 1024))
+    send(12, None, v("X", 0, 2048), v("X", 0, 2048))
+    send(5, rank - 3, v("WE2", 0, 2048), v("WD", 0, 2048))
+    arrive(6, v("FI0"), 6, 4.0)
+    arrive(0, v("XE0"), 0, 20.0)
+    arrive(3, v("WE0", 0, 1024), 3, 30.0)
+    arrive(14, v("WE0", 1024, 2048), 13, 30.0)
+    arrive(1, v("XE1"), 12, 40.0)
+    arrive(4, v("WE1", 0, 2048), 12, 60.0)
+    arrive(2, v("XE2"), 12, 80.0)
+    arrive(5, v("WE2", 0, 2048), 5, 70.0)
 
     def late_constants():
         ts(v("R2", 0, 143), v("R1", 0, 143), 2.0, A.mult)
         ts(v("RN", 0, 143), v("R1", 0, 143), -1.0, A.mult)
         act(v("R1f", 0, 143), v("R1", 0, 143))
         act(v("BOf"), v("BO"))
-        for n_, c_ in (("UW", "uw"), ("BOI", "ki"), ("BC", "c16")):
+        for n_, c_ in (("UD", "ud"), ("BOI", "ki"), ("BC", "c16")):
             act(v(n_), v("BO"), scale=col[c_])
-        for n_, c_ in (("D0", "q0"), ("D1", "q1"), ("X2D", "q2"), ("K34", "k34")):
+        for n_, c_ in (("D0", "q0"), ("D1", "q1"), ("K34", "keep")):
             act(v(n_), v("ID"), scale=col[c_])
+        ts(v("NI"), v("ID"), -1.0, A.mult)
+        ts(v("X2D"), v("CR", 0, 128), col["k5"], A.is_equal, col["q7"], A.mult)
+        tt(v("X2D"), v("X2D"), v("K34"), A.add)
 
     def last_constants():
         cp(v("thB", 0, 1), v("thi"))
@@ -495,34 +558,43 @@ def rank_program(g, core, T, topo):
         mms([(v("q5", 64, 96), win("RH", i), v("TBL", i, 512, 16)) for i in range(16)])
         cp(v("STu"), v("q5", 64, 96))
         gat(v("Ku"), v("RQ"), v("STu"))
+        sgat(v("KX"), v("RQ"), v("STu"), 8192.0)
+        sgat(v("W4"), v("WD"), v("Lu"), 4.0)
+
+    CH = (0, 160, 320, 448, 512)
 
     def check(t):
         def ch(x, k):
-            return v(x, 128 * k, 128 * k + 128)
+            return v(x, CH[k], CH[k + 1])
 
         def sig(k):
-            sgat(v("sg%d" % (k & 1)), v("SG"), ch("Ku", k))
+            sgat(tile("sg", k), v("SG"), ch("Ku", k))
+
+        def tile(x, k, p=None):
+            n = 16 * (CH[k + 1] - CH[k])
+            name = "%s%d" % (x, k & 1)
+            return v(name, 0, n) if p is None else v(name, p, n, 16)
 
         def typ(k, e):
-            (gat if e == "V" else sgat)(v("hg%d" % (k & 1)), v("TB"), ch("Wu", k))
+            (gat if e == "V" else sgat)(tile("hg", k), v("TB"), ch("Wu", k))
 
         def val(k):
-            gtt(v("mm%d" % (k & 1)), v("X"), ch("Wu", k), v("sg%d" % (k & 1)), A.max)
+            gtt(tile("mm", k), v("X"), ch("Wu", k), tile("sg", k), A.max)
 
         def sums(k):
-            q, h, s, m = "q%d" % (k & 1), "hg%d" % (k & 1), "sg%d" % (k & 1), "mm%d" % (k & 1)
-            mms([(v(q, 128, 256), win("RH", p), v(h, p, 2048, 16)) for p in range(16)])
-            mms([(v(q, 0, 128), win("RX", p), v(h, p, 2048, 16)) for p in range(16)],
-                [(v(q, 0, 128), win("RN", p), v(s, p, 2048, 16)) for p in range(16)],
-                [(v(q, 0, 128), win("R2", p), v(m, p, 2048, 16)) for p in range(16)])
+            q, n = ("q0", "q1", "q7", "q0")[k], CH[k + 1] - CH[k]
+            parts = [[(v(q, 0, n), win(R, p), tile(x, k, p)) for p in range(16)] for R, x in (("RX", "hg"), ("RN", "sg"), ("R2", "mm"))]
+            mms(*(parts if k < 3 else (parts[1], parts[0], parts[2])))
 
         def small(k):
-            q = "q%d" % (k & 1)
-            tt(v("O0"), v(q, 128, 256), ch("Kf", k), A.not_equal)
-            ts(v("GA"), v(q, 0, 128), v("thB", 1, 2), A.is_gt, 2.0, A.add)
-            tt(ch("OT", k), v("O0"), ch("PM", k), A.mult)
-            tt(ch("FO", k), ch("OT", k), v("GA"), A.mult)
-            tt(ch("P1", k), ch("W4K", k), ch("FO", k), A.add)
+            q, n = ("q0", "q1", "q7", "q0")[k], CH[k + 1] - CH[k]
+            tt(v("ED", 0, n), v(q, 0, n), ch("KX", k), A.subtract)
+            ts(v("ED", 160, 160 + n), v("ED", 0, n), 8191, A.bitwise_and)
+            tt(v("O0", 0, n), v("ED", 160, 160 + n), v("ED", 0, n), A.not_equal)
+            ts(v("GA", 0, n), v("ED", 160, 160 + n), v("thB", 1, 2), A.is_gt, 2.0, A.add)
+            tt(v("FT", 512 + CH[k], 512 + CH[k + 1]), v("O0", 0, n), ch("PM", k), A.mult)
+            tt(ch("FT", k), v("FT", 512 + CH[k], 512 + CH[k + 1]), v("GA", 0, n), A.mult)
+            act(ch("FOf", k), ch("FT", k))
 
         sig(0)
         typ(0, "V")
@@ -533,21 +605,14 @@ def rank_program(g, core, T, topo):
         sig(1)
         typ(1, "S")
         ts(v("PM"), v("Ku"), 1024.0, A.is_lt)
-        cp(v("Kf"), v("Ku"))
         val(1)
         sums(1)
-        sgat(v("XL"), v("X"), v("Lu"))
         sig(2)
         typ(2, "S")
-        ts(v("KX"), v("Ku"), 8192.0, A.mult)
-        ts(v("W4K"), v("Wu"), 4.0, A.mult)
-        tt(v("W4K"), v("W4K"), v("KX"), A.add)
+        tt(v("W4K"), v("W4"), v("KX"), A.add)
         small(0)
-        mms([(v("q6"), v("BC"), v("CC")), (v("q6"), v("BOI"), v("OH"))])
-        mms([(v("q7"), v("UW"), v("XL"))])
-        cp(v("UI"), v("q7"))
-        ts(v("UI"), v("UI"), 2047 << 12, A.bitwise_and)
-        tt(v("P2"), v("q6"), v("UI"), A.add)
+        mms([(v("q6"), v("BC"), v("CC")), (v("q6"), v("BOI"), v("OH")), (v("q6"), v("UD"), v("TBL"))])
+        act(v("P2"), v("q6"), F.Identity, bias=float(896 * t % 2048))
         val(2)
         sums(2)
         sig(3)
@@ -559,7 +624,7 @@ def rank_program(g, core, T, topo):
         ts(v("HLi", 32, 64), v("TY", 0, 32), 5.0, A.mult)
         tt(v("TY", 32, 64), v("HLi", 0, 32), v("HLi", 32, 64), A.add)
         ms(v("P1W", 0, 192), 0.0)
-        ms(v("P2W", 0, 128), 2048.0)
+        ms(v("P2W", 0, 128), 8388608.0)
         ms(v("CW", 0, 512), 0.0)
         val(3)
         sums(3)
@@ -570,8 +635,7 @@ def rank_program(g, core, T, topo):
         last = t == 2
         c16 = 896 * t % 2048
         lw = lambda k: v("LW", 32 * k, 32 * k + 32)
-        mms([(v("q3", 32, 64), win("R1", i), v("OT", i, 512, 16)) for i in range(16)])
-        mms([(v("q3", 0, 32), win("R1", i), v("FO", i, 512, 16)) for i in range(16)])
+        mms([(v("q3", 0, 64), win("R1", i), v("FT", i, 1024, 16)) for i in range(16)])
         ts(lw(0), v("q3", 32, 64), -2.0, A.mult)
         tt(lw(1), v("q3", 0, 32), lw(0), A.add)
         ts(lw(4), lw(0), -1.0, A.is_lt)
@@ -581,7 +645,7 @@ def rank_program(g, core, T, topo):
         tt(v("RP", 32, 64), lw(4), lw(2), A.mult)
         mms([(v("q4", 0, 64), v("BO"), v("RP"))])
         mms([(v("q4", 64, 128), v("LPB"), v("RP"))])
-        mm = [(v("q6"), v("K34"), v("TBL")), (v("q6"), v("X2D"), v("XL"))]
+        mm = [(v("q6"), v("X2D"), v("TBL"))]
         tt(v("HLi", 64, 96), v("TY", 32, 64), lw(1), A.add)
         scan(lw(5), v("q4", 0, 32), v("ZF", 0, 32), A.add)
         scan(lw(6), v("q4", 32, 64), v("ZF", 0, 32), A.add)
@@ -598,7 +662,8 @@ def rank_program(g, core, T, topo):
         tt(lw(9), lw(9), v("J192"), A.add)
         tt(v("HLi", 64, 96), v("HLi", 64, 96), v("TY", 0, 32), A.add)
         cp(v("PFu"), lw(9))
-        sca(v("P1W"), v("PFu"), v("P1"))
+        op("V", lambda: g.vector.tensor_tensor(ind(v("P1W"), v("PFu")), ap(v("W4K")), ap(v("FOf")), A.add),
+           [v("W4K"), v("FOf"), v("PFu")], [v("P1W")], ew(512, 3.5))
         ts(v("HLi", 128, 160), v("HLi", 64, 96), 5, A.arith_shift_right)
         ts(v("HLi", 160, 192), v("HLi", 64, 96), 31, A.bitwise_and)
         cp(v("HLb"), v("HLi", 128, 192))
@@ -616,24 +681,26 @@ def rank_program(g, core, T, topo):
         ts(af(0, 64), v("q4", 0, 64), 0.5, A.is_lt)
         tt(af(0, 64), af(0, 64), ab(0, 64), A.mult)
         tt(af(64, 128), v("P1W", 128, 192), af(0, 64), A.mult)
-        mms([(v("q4", 64, 68), win("R1f", i), v("AF", 64 + i, 128, 16)) for i in range(16)])
         mms([(v("q4", 0, 64), v("BOf"), af(64, 128))])
-        mms(mm[:2], mm[2:])
+        mms(mm[:1], mm[1:])
         act(v("TBn"), v("q6"), F.Identity, bias=col["b2"])
         bi = lambda k: v("BI", 128 * k, 128 * k + 128)
         cp(bi(0), v("P2W", 0, 128))
-        cp(ai(128, 196), v("q4", 0, 68))
+        tt(af(216, 280), v("q4", 0, 64), v("EQ0", 0, 64), A.mult)
+        cp(ai(128, 192), v("q4", 0, 64))
+        tt(af(280, 312), v("AF", 216, 280, 2), v("AF", 217, 280, 2), A.add)
+        tt(af(312, 328), v("AF", 280, 312, 2), v("AF", 281, 312, 2), A.add)
+        tt(af(328, 336), v("AF", 312, 328, 2), v("AF", 313, 328, 2), A.add)
+        tt(ai(192, 196), v("AF", 328, 336, 2), v("AF", 329, 336, 2), A.add)
         ts(bi(1), bi(0), 2047, A.bitwise_and)
         ts(ai(196, 264), ai(128, 196), 2, A.arith_shift_right, 2047, A.bitwise_and)
-        if c16:
-            ts(bi(1), bi(1), float(c16), A.add)
-            ts(bi(1), bi(1), 2047, A.bitwise_and)
         cp(af(128, 196), ai(196, 264))
         cp(v("AU", 0, 4), ai(260, 264))
         cp(v("BU", 0, 128), bi(1))
         sgat(ab(320, 384), v("SXT"), v("AU", 0, 4))
-        sgat(v("sg0"), v("X"), v("BU", 0, 128))
-        ts(bi(2), bi(0), 12, A.arith_shift_right)
+        for h in (0, 1):
+            sgat(v("sg0", 1024 * h, 1024 * h + 1024), v("X"), v("BU", 64 * h, 64 * h + 64))
+        ts(bi(2), bi(0), 12, A.arith_shift_right, 2047, A.bitwise_and)
         for c in range(4):
             ts(ab(64 + 64 * c, 128 + 64 * c), af(128, 192), af(192 + c, 193 + c), A.is_equal)
         tt(bi(3), bi(2), bi(2), A.mult)
@@ -641,7 +708,7 @@ def rank_program(g, core, T, topo):
         tt(ab(64, 320), ab(64, 320), v("MK"), A.mult)
         ts(bi(3), bi(3), 5, A.arith_shift_right)
         for c in range(4):
-            red(af(200 + c, 201 + c), ab(64 + 64 * c, 128 + 64 * c))
+            act(ab(64 + 64 * c, 128 + 64 * c), ab(64 + 64 * c, 128 + 64 * c), accum_out=af(200 + c, 201 + c))
         tt(bi(3), bi(3), bi(4), A.add)
         ts(ai(264, 268), ai(192, 196), 2, A.bitwise_and)
         ts(bi(3), bi(3), 2047, A.bitwise_and)
@@ -655,14 +722,14 @@ def rank_program(g, core, T, topo):
         tt(af(204, 208), af(204, 208), af(192, 196), A.max)
         cp(ab(384, 512), ai(272, 400))
         cp(v("AU", 4, 8), af(204, 208))
-        mms([(v("q2", 0, 64), v("ID"), ab(320, 384)), (v("q2", 0, 64), v("D0"), ab(384, 448)), (v("q2", 0, 64), v("D1"), ab(448, 512))])
+        mms([(v("q2", 0, 64), v("K34"), ab(320, 384)), (v("q2", 0, 64), v("D0"), ab(384, 448)), (v("q2", 0, 64), v("D1"), ab(448, 512))])
         act(ab(512, 576), v("q2", 0, 64), F.Identity, bias=col["b2"])
         sca(v("TB"), v("Lu"), v("TBn"))
         sca(v("TB"), v("AU", 4, 8), ab(512, 576))
         if not last:
             dma("Y", v("FL%d" % (t + 1)), v("TB", 0, 2048, 1, slice(2, 128, 16)))
             send(7 + t, rank - 2 - t, v("FI%d" % (t + 1)), v("FL%d" % (t + 1)))
-            arrive(7 + t, rank + 2 + t, v("FI%d" % (t + 1)))
+            arrive(7 + t, v("FI%d" % (t + 1)), 7 + t, 4.0)
             ts(v("EX", 0, 32), v("EX", 0, 32), 0.5, A.is_lt)
             tt(v("EX", 0, 32), v("EX", 0, 32), lw(2), A.mult)
             red(v("thB", 2, 3), v("EX", 0, 32))
@@ -680,24 +747,24 @@ def rank_program(g, core, T, topo):
         sm = lambda k: v("BI", 1024 + 8 * k, 1032 + 8 * k)
         xe, c16 = "XE%d" % t, 896 * t % 2048
         mms([(v("q5", 0, 8), win("R0f", i), v("P2W", i, 128, 16)) for i in range(16)])
-        gtt(v("mm0"), v(xe), v("BU", 128, 256), v("sg0"), A.subtract)
-        act(v("hg0"), v("mm0"), F.Abs)
-        mms([(v("q7", 0, 128), win("R1", m), v("hg0", m, 2048, 16)) for m in range(16)])
+        for h in (0, 1):
+            sgat(v("mm0", 1024 * h, 1024 * h + 1024), v(xe), v("BU", 128 + 64 * h, 192 + 64 * h))
+            for b in (2 * h, 2 * h + 1):
+                q, lo, hi = "q%d" % (b & 1), 512 * b, 512 * b + 512
+                mms([(v(q), v("NI"), v("sg0", lo, hi)), (v(q), v("ID"), v("mm0", lo, hi))])
+                act(v("hg0", lo, hi), v(q), F.Abs)
+            mms([(v("q7", 64 * h, 64 * h + 64), win("R1", m), v("hg0", 1024 * h + m, 1024 * h + 1024, 16)) for m in range(16)])
         cp(sm(0), v("q5", 0, 8))
         cp(bi(4), v("P1W", 0, 128))
         ts(sm(1), sm(0), 2047, A.bitwise_and)
-        ts(sm(2), sm(0), 12, A.arith_shift_right)
+        ts(sm(2), sm(0), 12, A.arith_shift_right, 2047, A.bitwise_and)
         ts(bi(5), bi(4), 1, A.bitwise_and)
         ts(bi(6), bi(4), 2, A.arith_shift_right, 2047, A.bitwise_and)
         tt(sm(3), sm(2), sm(2), A.mult)
         ts(sm(4), sm(2), 2.0, A.mult, 1.0, A.add)
-        if c16:
-            ts(sm(1), sm(1), float(c16), A.add)
-            ts(sm(1), sm(1), 2047, A.bitwise_and)
         ts(sm(3), sm(3), 5, A.arith_shift_right)
-        ts(sm(5), sm(0), 2048, A.bitwise_and)
         tt(sm(3), sm(3), sm(2), A.add)
-        ts(bf(520, 528), sm(5), 0.5, A.is_gt)
+        ts(bf(520, 528), sm(0), 8388608.0, A.is_ge)
         ts(bf(0, 128), v("q7", 0, 128), 16.0, A.mult, kif, A.add)
         op("V", lambda: g.vector.transpose(ap(bf(128, 256)), ap(bf(0, 128))), [bf(0, 128)], [bf(128, 256)])
         lo, n, o = 128, 128, 256
@@ -718,28 +785,25 @@ def rank_program(g, core, T, topo):
         ts(sm(7), sm(7), 2047, A.bitwise_and)
         cp(v("BU", 264, 272), v(dw, 128, 136))
         cp(v("BU", 256, 264), sm(7))
-        gat(bi(7), v("WDE"), v("BU", 256, 264))
-        tt(bi(7), bi(7), bi(6), A.subtract)
-        tt(bi(7), bi(7), bi(5), A.mult)
-        tt(v(dw, 0, 128), bi(7), bi(6), A.add)
-        if t == 2:
-            cp(v("BF2", 0, 128), v(dw, 0, 128))
-            sca(v("YM"), v("BU", 264, 272), v("BF2", 0, 128))
-            fin.append(dma("Y", None, v("YM", 0, 2048), o=T.ym[:]))
-            return
+        gat(bf(384, 512), v("WE%d" % t), v("BU", 256, 264))
+        tt(bf(384, 512), bf(384, 512), bi(6), A.subtract)
+        tt(bf(384, 512), bf(384, 512), bi(5), A.mult)
+        tt(v(dw, 0, 128), bf(384, 512), bi(6), A.add)
         sca(v("WD"), v("BU", 264, 272), v(dw, 0, 128))
+        if t == 2:
+            fin.append(dma("Y", None, v("WD", 0, 2048), o=T.ym[:]))
+            return
         for t2 in range(t + 1, 3):
             slot = 9 + t + t2 - 1
             send(slot, rank - 1 - t2, v("Di%d%d" % (t, t2)), v(dw))
-            arrive(slot, rank + 1 + t2, v("Di%d%d" % (t, t2)))
+            arrive(slot, v("Di%d%d" % (t, t2)), slot, 4.0)
 
     def helper(t):
         dma("Y", v("XE%d" % t, 0, 2048, 1, slice(2, 128, 16)), v("FI%d" % t))
-        cp(v("WDE", 0, 2048), v("WE%d" % t))
         for s in range(t):
             b = "Di%d%d" % (s, t)
             cp(v("BU", 272, 280), v(b, 128, 136))
-            sca(v("WDE"), v("BU", 272, 280), v(b, 0, 128))
+            sca(v("WE%d" % t), v("BU", 272, 280), v(b, 0, 128))
 
     def flags_out():
         mms([(v("q2", 0, 128), win("RH", b), v("TB", 128 * b, 128 * b + 128)) for b in range(16)])
@@ -755,8 +819,6 @@ def rank_program(g, core, T, topo):
         fetch(t)
         check(t)
         helper(t)
-        if t == 2:
-            cp(v("YM"), v("WD"))
         post(t)
         if t == 2:
             flags_out()

from concourse.mybir import AluOpType as A, AxisListType, ActivationFunctionType as F

PATIENCE = 0.5
SCRATCH = {}
SEMAPHORES = ["cV", "cS", "cP", "cG"]


PLACE = {}
_POOLED = ("BO", "LT", "EQ0", "GT", "ID", "TRI", "LPA", "LPB", "UW", "BOI", "BC", "ON", "D0", "D1", "X2D", "K34", "R1", "RD0", "RI",
           "RC", "RH", "RX", "RD2", "R2", "RN", "RH12", "C1", "MK", "COLS", "CR", "MG", "MI", "BOf", "R1f", "R0f", "SW", "W8", "JW",
           "J192", "DD", "LIM", "JC", "NI", "RU", "RH8", "UD")


def _buf(name, cols, dtype, where="sbuf"):
    if name in _POOLED:
        pool = "PB" if dtype == "bfloat16" else "PF"
        at = SCRATCH[pool][1][1] if pool in SCRATCH else 0
        PLACE[name] = (pool, at, cols, dtype)
        SCRATCH[pool] = ("sbuf", [128, at + (cols + 15) // 16 * 16], dtype)
    else:
        PLACE[name] = (name, 0, cols, dtype)
        SCRATCH[name] = (where, [128, cols], dtype)


for _n, _c, _d in (
        ("X", 2560, "bfloat16"), ("WD", 2560, "float32"), ("RQ", 1032, "float32"), ("SG", 1040, "bfloat16"),
        ("TB", 2640, "bfloat16"), ("SXT", 2048, "bfloat16"), ("WI", 2048, "int32"), ("RI32", 1024, "int32"), ("NI", 128, "bfloat16"),
        ("FOf", 512, "float32"), ("RU", 144, "bfloat16"), ("UD", 128, "bfloat16"),
        ("hyb", 128, "int32"), ("vfb", 128, "int32"), ("x2b", 128, "bfloat16"),
        ("thi", 1, "int32"), ("KI", 4, "int32"), ("COLS", 32, "float32"), ("CR", 256, "float32"), ("MG", 128, "float32"),
        ("MI", 128, "float32"), ("BO", 128, "bfloat16"), ("BOf", 128, "float32"), ("LT", 128, "bfloat16"), ("EQ0", 128, "bfloat16"),
        ("GT", 128, "bfloat16"), ("ID", 128, "bfloat16"), ("TRI", 128, "bfloat16"), ("LPA", 128, "bfloat16"), ("LPB", 128, "bfloat16"),
        ("UW", 128, "bfloat16"), ("BOI", 128, "bfloat16"), ("BC", 128, "bfloat16"), ("ON", 128, "bfloat16"),
        ("D0", 128, "bfloat16"), ("D1", 128, "bfloat16"), ("X2D", 128, "bfloat16"), ("K34", 128, "bfloat16"),
        ("R1", 144, "bfloat16"), ("RD0", 144, "bfloat16"), ("RI", 144, "bfloat16"), ("RC", 144, "bfloat16"), ("RH", 144, "bfloat16"),
        ("RX", 144, "bfloat16"), ("RD2", 144, "bfloat16"), ("R2", 144, "bfloat16"), ("RN", 144, "bfloat16"),
        ("R1f", 144, "float32"), ("R0f", 144, "float32"), ("SW", 512, "float32"), ("RH12", 16, "bfloat16"),
        ("W8", 24, "float32"), ("C1", 128, "bfloat16"), ("JI", 512, "float32"), ("JW", 32, "float32"), ("J192", 32, "float32"), ("DD", 64, "float32"),
        ("LIM", 64, "float32"), ("JC", 64, "float32"), ("MK", 256, "bfloat16"), ("ZR", 512, "bfloat16"), ("ZF", 128, "float32"),
        ("U0", 2064, "bfloat16"), ("UH", 2048, "bfloat16"), ("UL", 2048, "bfloat16"), ("UG", 2048, "bfloat16"),
        ("NW", 128, "bfloat16"), ("CUM", 128, "float32"), ("POS", 128, "float32"), ("TTB", 384, "bfloat16"),
        ("OF", 24, "float32"), ("OFu", 8, "uint16"), ("CW", 4352, "bfloat16"), ("CC", 512, "bfloat16"), ("CLu", 32, "uint16"),
        ("OH", 512, "bfloat16"), ("EX", 64, "float32"), ("Li", 64, "int32"), ("Lu", 32, "uint16"), ("TBL", 512, "bfloat16"),
        ("Wu", 512, "uint16"), ("Ku", 512, "uint16"), ("STu", 32, "uint16"), ("TY", 64, "int32"),
        ("PM", 512, "bfloat16"), ("W4", 512, "float32"), ("W4K", 512, "float32"), ("KX", 512, "float32"),
        ("P2", 512, "float32"), ("FT", 1024, "bfloat16"),
        ("ED", 320, "int32"), ("GA", 160, "bfloat16"), ("O0", 160, "bfloat16"),
        ("sg0", 2560, "bfloat16"), ("sg1", 2560, "bfloat16"), ("mm0", 2560, "bfloat16"), ("mm1", 2560, "bfloat16"),
        ("hg0", 2560, "bfloat16"), ("hg1", 2560, "bfloat16"),
        ("LW", 416, "float32"), ("HLi", 192, "int32"), ("HLb", 64, "bfloat16"), ("RP", 64, "bfloat16"), ("GM", 32, "bfloat16"),
        ("PFu", 32, "uint16"), ("P1W", 704, "float32"), ("P2W", 704, "float32"), ("TBn", 512, "bfloat16"), ("thB", 4, "float32"),
        ("CN", 4, "int32"), ("AI", 512, "int32"), ("AF", 640, "float32"), ("AB", 704, "bfloat16"), ("AU", 8, "uint16"),
        ("BI", 1200, "int32"), ("BF2", 560, "float32"), ("BU", 320, "uint16"), ("FL0", 128, "bfloat16"), ("FL1", 128, "bfloat16"),
        ("FL2", 128, "bfloat16"), ("DW0", 136, "float32"), ("DW1", 136, "float32"), ("DW2", 136, "float32")):
    _buf(_n, _c, _d)
for _t in range(3):
    _buf("XE%d" % _t, 2048, "bfloat16")
    _buf("WE%d" % _t, 2176, "float32")
    _buf("FI%d" % _t, 128, "bfloat16")
for _n in ("i01", "i02", "i12"):
    _buf("D" + _n, 136, "float32")
for _b in range(8):
    _buf("q%d" % _b, 512, "float32", "psum")
_NDMA, _NREM = 40, 15
SEMAPHORES += ["d%d" % k for k in range(_NDMA)] + ["l%d" % k for k in range(_NREM)] + ["r%d" % k for k in range(_NREM)]


def relay_of(core, T, topo):
    return [c for c in topo.cores_of(core) if T.rank_of(c) is None and topo.die(c) != topo.die(core)
            and all(topo.may_write(c, d) for d in T.cores)][0]


def lanes_of(src, dst, T, topo):
    far = [d for d in T.cores if topo.chip(d) != topo.chip(src)][0]
    e = [k for k in topo.engines(src, dst) if k in topo.engines(src, far)]
    return sum(1 << k for k in e), len(e)


def relay_program(g, core, T, topo):
    own = [c for c in T.cores if topo.chip(c) == topo.chip(core)]
    if not own or relay_of(own[0], T, topo) != core:
        return
    rank, sent = T.rank_of(own[0]), []
    n_on = lanes_of(own[0], core, T, topo)[1]
    for slot, d, name, lo, hi, src in ((14, 1, "WE0", 1024, 2048, "WD"), (1, 2, "XE1", 0, 2048, "X"), (4, 2, "WE1", 0, 2048, "WD"), (2, 3, "XE2", 0, 2048, "X")):
        if slot == 14:
            g.wait_ge(T.sem.r13, n_on)
        if slot == 1:
            g.wait_ge(T.sem.r12, n_on)
        dst = T.cores[(rank - d) % len(T.cores)]
        mask, n = lanes_of(core, dst, T, topo)
        rid, pid, _ = topo.addr(dst)
        g.remote_dma(T[name][:, lo:hi], T[src][:, lo:hi], T.sem["r%d" % slot], T.sem["l%d" % slot], pid, rid, mask)
        sent.append((slot, n))
    for slot, n in sent:
        g.wait_ge(T.sem["l%d" % slot], n)


def rank_program(g, core, T, topo):
    rank = T.rank_of(core)
    if rank is None:
        relay_program(g, core, T, topo)
        return
    N = len(T.cores)
    GQ = ("gq", 0, 1, 1, None)
    eng = {"V": g.vector, "S": g.scalar, "P": g.tensor, "G": g, "Y": g.sync}
    cnt = {"cV": 0, "cS": 0, "cP": 0, "cG": 0}
    known = {e: {} for e in eng}
    acc = {}
    nd, sent, fin = [0], [], []
    psum = {"q%d" % b for b in range(8)}

    def v(name, lo=0, hi=None, step=1, rows=None):
        buf, at, cols, _ = PLACE[name]
        return (buf, at + lo, at + (cols if hi is None else hi), step, rows)

    def ap(x):
        name, lo, hi, step, rows = x
        r = slice(None) if rows is None else rows
        return T[name][r, lo:hi] if step == 1 else T[name][r, lo:hi:step]

    def wait(e, sem, val, clock):
        k = known[e]
        if k.get(sem, 0) < val:
            eng[e].wait_ge(T.sem[sem], val)
            k[sem] = val
        for s, c in clock.items():
            if k.get(s, 0) < c:
                k[s] = c

    def deps(e, reads, writes):
        need = []
        for lst, wr in ((reads, False), (writes, True)):
            for x in lst:
                ex = x[0] in psum
                for a in acc.get(x[0], ()):
                    if ex and e == "P" and a[4] == "P":
                        continue
                    if ex and a[4] != e:
                        need.append(a)
                    elif a[1] < x[2] and x[1] < a[2] and (wr or a[3]) and (a[0] is None or x[4] is None or a[0] == x[4]):
                        need.append(a)
        need.sort(key=lambda a: -a[6])
        for a in need:
            wait(e, a[5], a[6], a[7])

    def note(e, reads, writes, sem, val, clock):
        for lst, wr in ((reads, False), (writes, True)):
            for x in lst:
                old = acc.setdefault(x[0], [])
                if x[0] in psum:
                    keep = [a for a in old if a[4] == e and not (wr and x[1] <= a[1] and a[2] <= x[2])]
                elif wr and x[3] == 1:
                    keep = [a for a in old if not (x[1] <= a[1] and a[2] <= x[2] and (x[4] is None or a[0] == x[4]))]
                else:
                    keep = [a for a in old if a[3] or a[4] != e or a[1:3] != (x[1], x[2]) or a[0] != x[4] or wr]
                keep.append((x[4], x[1], x[2], wr, e, sem, val, clock))
                acc[x[0]] = keep

    prog = []

    def call(e, emit, reads, writes, cost, lat=0.0):
        prog.append({"e": e, "emit": emit, "r": reads, "w": writes, "cost": cost, "lat": lat})

    def op(e, fn, reads, writes, cost=0.1):
        def emit():
            deps(e, reads, writes)
            sem = "c" + e
            cnt[sem] += 1
            fn().then_inc(T.sem[sem], 1)
            clock = dict(known[e])
            clock[sem] = cnt[sem]
            note(e, reads, writes, sem, cnt[sem], clock)
        call(e, emit, reads, writes, cost)

    def mms(*parts):
        for n, lst in enumerate(parts):
            first, last = n == 0, n == len(parts) - 1
            cyc = sum(max(64, (r[2] - r[1]) // r[3]) * (4 if r[0] in ("AF", "BF2", "P2W") else 1) for _, _, r in lst)

            def emit(lst=lst, first=first, last=last):
                sem = "cP"
                val = cnt[sem] + 1
                for k, (o, l, r) in enumerate(lst):
                    deps("P", [l, r], [o] if k == 0 else [])
                    m = g.tensor.matmul(ap(o), ap(l), ap(r), first and k == 0, last and k == len(lst) - 1)
                m.then_inc(T.sem[sem], 1)
                cnt[sem] = val
                clock = dict(known["P"])
                clock[sem] = val
                note("P", [x[1] for x in lst] + [x[2] for x in lst], [x[0] for x in lst], sem, val, clock)
            call("P", emit, [x[1] for x in lst] + [x[2] for x in lst], [x[0] for x in lst], cyc * 0.7e-3)

    def dma(e, out, in_, o=None, i=None):
        sem = "d%d" % nd[0]
        nd[0] += 1
        rd, wr = ([] if in_ is None else [in_]), ([] if out is None else [out])

        def emit():
            deps(e, rd, wr)
            eng[e].dma_start(ap(out) if o is None else o, ap(in_) if i is None else i).then_inc(T.sem[sem], 16)
            clock = dict(known[e])
            clock[sem] = 16
            note("D" + sem, rd, wr, sem, 16, clock)
        big = (out or in_)[4] is None and (out or in_)[2] - (out or in_)[1] > 512
        call(e, emit, rd, wr, 0.06, 5.0 if big else 2.3)
        return sem

    def send(slot, to, out, in_):
        dst = relay_of(core, T, topo) if to is None else T.cores[to % N]
        mask, n = lanes_of(core, dst, T, topo)
        sent.append(("l%d" % slot, n))

        def emit():
            deps("G", [in_], [])
            rid, pid, _ = topo.addr(dst)
            g.remote_dma(ap(out), ap(in_), T.sem["r%d" % slot], T.sem["l%d" % slot], pid, rid, mask)
            note("Dl%d" % slot, [in_], [], "l%d" % slot, n, {"l%d" % slot: n})
        call("G", emit, [in_], [(slot, 0, 1, 1, None), GQ], 1.2, 0.0)

    def arrive(slot, buf, left, way):
        n = lanes_of(T.cores[(rank + 1) % N], core, T, topo)[1]
        call("R", lambda: note("Dr%d" % slot, [], [buf], "r%d" % slot, n, {"r%d" % slot: n}), [(left, 0, 1, 1, None)], [buf], way)

    def issue():
        hist, pred = {}, []
        for k, c in enumerate(prog):
            ps = {}
            for lst, wr in ((c["r"], False), (c["w"], True)):
                for x in lst:
                    h = hist.setdefault(x[0], [])
                    for a in h:
                        if a[0] == k:
                            continue
                        if x[0] in psum:
                            hit = wr or a[4] or a[5] != c["e"]
                        else:
                            hit = (wr or a[4]) and a[1] < x[2] and x[1] < a[2] and (a[3] is None or x[4] is None or a[3] == x[4])
                        if hit:
                            ps[a[0]] = max(ps.get(a[0], 0.0), 0.0 if x == GQ else prog[a[0]]["lat"] + 0.1)
            for lst, wr in ((c["r"], False), (c["w"], True)):
                for x in lst:
                    h = hist[x[0]]
                    if wr and x[3] == 1:
                        if x[0] in psum:
                            h[:] = [a for a in h if a[0] == k]
                        else:
                            h[:] = [a for a in h if not (x[1] <= a[1] and a[2] <= x[2] and (x[4] is None or a[3] == x[4]))]
                    e = (k, x[1], x[2], x[4], wr, c["e"])
                    if e not in h:
                        h.append(e)
            pred.append(ps)
        n = len(prog)
        rank_, succ = [0.0] * n, [[] for _ in range(n)]
        for k in range(n):
            for p in pred[k]:
                succ[p].append(k)
        for k in range(n - 1, -1, -1):
            rank_[k] = prog[k]["cost"] + max([rank_[s] + pred[s][k] for s in succ[k]] or [0.0])
        left = [len(p) for p in pred]
        at, free, done = [0.0] * n, {}, [0.0] * n
        ready = {k for k in range(n) if left[k] == 0}
        while ready:
            best = None
            for k in ready:
                e = prog[k]["e"]
                t0 = at[k] if e == "R" else max(at[k], free.get(e, 0.0))
                key = (t0, -rank_[k], k)
                if best is None or key < best:
                    best = key
            t0, _, k = best
            e, late = prog[k]["e"], t0 + PATIENCE * prog[k]["cost"]
            if e in ("V", "S", "P"):
                for j in ready:
                    if prog[j]["e"] == e and at[j] < late and (rank_[j], -j) > (rank_[k], -k):
                        k = j
                t0 = max(at[k], free.get(e, 0.0))
            ready.remove(k)
            c = prog[k]
            c["emit"]()
            done[k] = t0 + c["cost"]
            free[c["e"]] = done[k]
            for s in succ[k]:
                at[s] = max(at[s], done[k] + pred[s][k])
                left[s] -= 1
                if left[s] == 0:
                    ready.add(s)

    def wid(x):
        return (x[2] - x[1] + x[3] - 1) // x[3]

    def half(*xs):
        return 0.5 if all(x[0] in two for x in xs) else 1.0

    two = {p[0] for p in PLACE.values() if p[3] in ("bfloat16", "uint16")}

    def ew(w, f=1.0):
        return 0.03 + max(64, w * f) * 1.04e-3

    def ind(win, off):
        return ap(win).indirect(ap(off))

    def tt(o, a, b, f):
        k = 1 if a[0] in psum or b[0] in psum else 2 * half(o, a, b)
        op("V", lambda: g.vector.tensor_tensor(ap(o), ap(a), ap(b), f), [a, b], [o], ew(wid(o), k))

    def ts(o, a, s1, f, s2=None, f2=None):
        rd = [a] + [x for x in (s1, s2) if isinstance(x, tuple)]
        p1 = ap(s1) if isinstance(s1, tuple) else s1
        p2 = ap(s2) if isinstance(s2, tuple) else s2
        w = ew(wid(o), half(o, a))
        if f2 is None:
            op("V", lambda: g.vector.tensor_scalar(ap(o), ap(a), p1, None, f), rd, [o], w)
        else:
            op("V", lambda: g.vector.tensor_scalar(ap(o), ap(a), p1, p2, f, f2), rd, [o], w)

    def cp(o, a):
        op("V", lambda: g.vector.tensor_copy(ap(o), ap(a)), [a], [o], ew(wid(o), half(o, a)))

    def ms(o, c):
        op("V", lambda: g.vector.memset(ap(o), c), [], [o], ew(wid(o), half(o)))

    def red(o, a):
        op("V", lambda: g.vector.tensor_reduce(ap(o), ap(a), AxisListType.X, A.add), [a], [o], ew(wid(a)))

    def asel(o, a, pattern, base):
        op("G", lambda: g.affine_select(ap(o), ap(a), pattern, A.is_equal, 0.0, base, 1), [a], [o, GQ], 0.2 + 2.1e-3 * wid(o))

    def gat(o, win, off):
        op("V", lambda: g.vector.tensor_copy(ap(o), ind(win, off)), [win, off], [o], ew(wid(o), 1.5))

    def sca(win, off, a):
        op("V", lambda: g.vector.tensor_copy(ind(win, off), ap(a)), [a, off], [win], ew(wid(a), 3.5))

    def gtt(o, win, off, b, f):
        op("V", lambda: g.vector.tensor_tensor(ap(o), ind(win, off), ap(b), f), [win, off, b], [o], ew(wid(o), 1.6))

    def scan(o, a, z, f):
        w = ew(wid(o), half(o, a))
        op("V", lambda: g.vector.tensor_tensor_scan(ap(o), ap(a), ap(z), 0.0, f, A.add), [a, z], [o], w)

    def act(o, a, func=F.Copy, bias=None, scale=None, accum_out=None):
        kw = {}
        rd = [a]
        for k, x in (("bias", bias), ("scale", scale)):
            if isinstance(x, tuple):
                rd += [x]
                kw[k] = ap(x)
            elif x is not None:
                kw[k] = x
        if accum_out is not None:
            kw["accum_out"] = ap(accum_out)
        op("S", lambda: g.scalar.activation(ap(o), ap(a), func, **kw), rd, [o] + ([] if accum_out is None else [accum_out]), ew(wid(o)))

    def sgat(o, win, off, scale=1.0):
        op("S", lambda: g.scalar.activation(ap(o), ind(win, off), F.Copy, scale=scale), [win, off], [o], ew(wid(o), 1.5))

    def iota(o, pattern, base, ch=0):
        if SCRATCH[o[0]][2] == "int32":
            op("G", lambda: g.iota(ap(o), pattern, base, ch), [], [o], 0.2)
        else:
            op("G", lambda: g.iota(ap(o), pattern, base, ch, allow_small_or_imprecise_dtypes=True), [], [o], 0.2 + 2.1e-3 * wid(o))

    def win(R, i):
        return v(R, 15 - i, 143 - i)

    dma("Y", v("vfb"), None, i=T.vf[:])
    dma("S", v("hyb"), None, i=T.hy[:])
    dma("Y", v("x2b"), None, i=T.xs[2:128:16, :])
    dma("S", v("X", 0, 2048), None, i=T.xs[:])
    dma("Y", v("WI"), None, i=T.wd[:])
    dma("S", v("RI32"), None, i=T.rq[:])
    dma("Y", v("SG", 0, 1024), None, i=T.sg[:])
    dma("S", v("thi"), None, i=T.th[:])

    iota(v("KI", 0, 1), [[1, 1]], 0, 1)
    iota(v("CR"), [[1, 256]], 0)
    iota(v("MG"), [[1, 8], [0, 16]], 0)
    iota(v("MI"), [[0, 8], [1, 16]], 0)
    iota(v("C1"), [[1, 128]], 0)
    iota(v("JI"), [[1, 512]], 4097)
    iota(v("JC", 0, 32), [[16, 32]], 0)
    col = {}

    def newcol(name):
        k = len(col)
        col[name] = v("COLS", k, k + 1)
        return col[name]

    ms(v("TB"), 0.0)
    kif, kgf, kf = newcol("ki"), newcol("kg"), newcol("k")
    ts(v("KI", 1, 2), v("KI", 0, 1), 4, A.arith_shift_right)
    ts(v("KI", 2, 3), v("KI", 0, 1), 15, A.bitwise_and)
    ts(v("KI", 3, 4), v("KI", 1, 2), 1, A.bitwise_and)
    cp(kif, v("KI", 2, 3))
    cp(kgf, v("KI", 1, 2))
    cp(kf, v("KI", 0, 1))
    odd, even = newcol("odd"), newcol("even")
    cp(odd, v("KI", 3, 4))
    ts(newcol("g15"), kgf, 16.0, A.mult, 15.0, A.add)
    for q in range(8):
        ts(newcol("q%d" % q), kif, float(q), A.is_equal)
    ts(even, odd, 0.0, A.is_equal)
    ts(newcol("c16"), col["q0"], 16.0, A.mult)
    ts(newcol("c32"), col["q0"], 32.0, A.mult)
    ts(newcol("x64"), col["q3"], -64.0, A.mult)
    ts(newcol("b2"), col["q2"], 8192.0, A.mult)
    ts(newcol("uw"), kif, 10.0, A.mult, 1.0, A.add)
    ts(newcol("u32"), col["q5"], 32.0 * 4096.0, A.mult)
    ts(newcol("u1"), col["q6"], 4096.0, A.mult)
    tt(newcol("ud"), col["u32"], col["u1"], A.add)
    ts(newcol("m2"), kif, 2.0, A.mult, 1.0, A.add)
    ts(newcol("km"), kf, -16.0, A.add)
    ts(newcol("kp"), kf, 16.0, A.add)
    ts(newcol("k5"), kf, -5.0, A.add)
    tt(newcol("h"), col["c32"], col["q1"], A.add)
    ts(newcol("keep"), kif, 2.5, A.is_gt)
    ts(newcol("sx"), col["h"], 8192.0, A.mult)
    tt(col["sx"], col["sx"], col["x64"], A.add)
    tt(col["sx"], col["sx"], col["q4"], A.subtract)
    ts(v("R1", 0, 143), v("CR", 0, 143), col["g15"], A.is_equal)
    ts(v("BI", 0, 128), v("hyb"), 5, A.arith_shift_right)
    ts(v("BI", 128, 256), v("hyb"), 31, A.bitwise_and)
    ts(v("BF2", 0, 128), v("vfb"), -8192.0, A.mult, 8192.0, A.add)
    tt(v("FL0"), v("BF2", 0, 128), v("x2b"), A.add)
    dma("Y", v("TB", 0, 2048, 1, slice(2, 128, 16)), v("FL0"))
    cp(v("AB", 0, 256), v("BI", 0, 256))
    dma("Y", v("TB", 0, 2048, 1, slice(0, 128, 16)), v("AB", 0, 128))
    dma("Y", v("TB", 0, 2048, 1, slice(1, 128, 16)), v("AB", 128, 256))
    ts(v("BO"), v("MG"), kgf, A.is_equal)
    ts(v("RD2", 0, 143), v("R1", 0, 143), col["q2"], A.mult)
    ts(v("GT"), v("MI"), kif, A.is_lt)
    ts(v("EQ0"), v("MI"), kif, A.is_equal)
    ts(v("LT"), v("MI"), kif, A.is_gt)
    tt(v("ID"), v("BO"), v("EQ0"), A.mult)
    tt(v("GT"), v("GT"), v("BO"), A.mult)
    ts(v("LPA"), v("ID"), 4096.0, A.mult)
    tt(v("LPA"), v("LPA"), v("GT"), A.subtract)
    ts(v("LPB"), v("ID"), -4096.0, A.mult)
    tt(v("LPB"), v("LPB"), v("GT"), A.subtract)
    ts(v("RH12", 0, 8), v("CR", 0, 8), kgf, A.is_gt)
    ts(v("RH12", 8, 16), v("CR", 0, 8), kgf, A.is_equal)
    ms(v("ZF"), 0.0)
    ms(v("ZR"), 0.0)
    ms(v("X", 2048, 2560), 0.0)
    ms(v("WD", 2048, 2560), 0.0)
    for t in range(3):
        ms(v("WE%d" % t, 2048, 2176), 0.0)
    ms(v("RQ", 1024, 1032), 1024.0)
    ms(v("SG", 1024, 1040), 0.0)
    ms(v("CW", 0, 512), 0.0)
    ts(v("TB", 2048, 2560), v("ZR"), col["c32"], A.add)
    ts(v("JW"), v("JC", 0, 32), kif, A.add)
    ts(v("W8", 0, 8), v("JW", 0, 8), 2048.0, A.add)
    ts(v("W8", 8, 12), v("JW", 0, 4), 2560.0, A.add)
    ts(v("JC", 32, 64), v("JW"), 2048.0, A.add)
    for n_, c_ in (("RD0", "q0"), ("RI", "ki"), ("RC", "c16"), ("RH", "h"), ("RX", "sx"), ("R0f", "q0"), ("RU", "uw")):
        act(v(n_, 0, 143), v("R1", 0, 143), scale=col[c_])
    dma("Y", v("TB", 0, 2048, 1, slice(7, 128, 16)), v("x2b"))
    mms([(v("q7", 0, 128), win("R1", b), v("X", 128 * b, 128 * b + 128)) for b in range(16)])
    mms([(v("q7", 128, 256), win("RU", b), v("X", 128 * b, 128 * b + 128)) for b in range(16)])
    cp(v("BI", 256, 512), v("q7", 0, 256))
    ts(v("BI", 512, 640), v("BI", 256, 384), 6, A.arith_shift_right)
    ts(v("BI", 640, 768), v("BI", 256, 384), 63, A.bitwise_and)
    ts(v("BI", 768, 896), v("BI", 384, 512), 5, A.arith_shift_right, 63, A.bitwise_and)
    ts(v("BI", 896, 1024), v("BI", 384, 512), 31, A.bitwise_and)
    cp(v("CW", 512, 1024), v("BI", 512, 1024))
    for q in range(3, 7):
        dma("Y", v("TB", 0, 2048, 1, slice(q, 128, 16)), v("CW", 128 * q + 128, 128 * q + 256))
    cp(v("SXT"), v("TB", 0, 2048))
    cp(v("RQ", 0, 1024), v("RI32"))
    cp(v("WD", 0, 2048), v("WI"))
    send(6, rank - 1, v("FI0"), v("FL0"))
    send(0, rank - 1, v("XE0"), v("X", 0, 2048))
    send(13, None, v("WD", 0, 2048), v("WD", 0, 2048))
    send(3, rank - 1, v("WE0", 0, 1024), v("WD", 0, 1024))
    send(12, None, v("X", 0, 2048), v("X", 0, 2048))
    send(5, rank - 3, v("WE2", 0, 2048), v("WD", 0, 2048))
    arrive(6, v("FI0"), 6, 4.0)
    arrive(0, v("XE0"), 0, 20.0)
    arrive(3, v("WE0", 0, 1024), 3, 30.0)
    arrive(14, v("WE0", 1024, 2048), 13, 30.0)
    arrive(1, v("XE1"), 12, 40.0)
    arrive(4, v("WE1", 0, 2048), 12, 60.0)
    arrive(2, v("XE2"), 12, 80.0)
    arrive(5, v("WE2", 0, 2048), 5, 70.0)

    def late_constants():
        ts(v("R2", 0, 143), v("R1", 0, 143), 2.0, A.mult)
        ts(v("RN", 0, 143), v("R1", 0, 143), -1.0, A.mult)
        act(v("R1f", 0, 143), v("R1", 0, 143))
        act(v("BOf"), v("BO"))
        for n_, c_ in (("UD", "ud"), ("BOI", "ki"), ("BC", "c16")):
            act(v(n_), v("BO"), scale=col[c_])
        for n_, c_ in (("D0", "q0"), ("D1", "q1"), ("K34", "keep")):
            act(v(n_), v("ID"), scale=col[c_])
        ts(v("NI"), v("ID"), -1.0, A.mult)
        ts(v("X2D"), v("CR", 0, 128), col["k5"], A.is_equal, col["q7"], A.mult)
        tt(v("X2D"), v("X2D"), v("K34"), A.add)

    def last_constants():
        cp(v("thB", 0, 1), v("thi"))
        cp(v("thB", 1, 2), v("thB", 0, 1))
        tt(v("TRI"), v("BO"), v("LT"), A.mult)
        ms(v("ON"), 1.0)
        ts(v("J192"), v("JW"), 192.0, A.add)
        ts(v("DD", 0, 32), v("JW"), 192.0 - 4095.0, A.add)
        ts(v("DD", 32, 64), v("JW"), 64.0 - 4095.0, A.add)
        ms(v("LIM", 0, 32), 128.0 - 4095.0)
        ms(v("LIM", 32, 64), 64.0 - 4095.0)
        for k, (c_, m_) in enumerate(((kf, even), (col["kp"], even), (col["km"], odd), (kf, odd))):
            ts(v("SW", 128 * k, 128 * k + 128), v("CR", 0, 128), c_, A.is_equal, m_, A.mult)
        for c in range(4):
            ts(v("AF", 64 * c, 64 * c + 64), v("CR", 0, 64), -1.0, A.mult, 16.0 * c - 0.5, A.add)
        ts(v("MK"), v("AF", 0, 256), kif, A.add, 0.0, A.is_gt)
        ms(v("U0"), 0.0)
        ms(v("U0", 0, 2064, 16), 1.0)
        for q, n_ in enumerate(("UH", "UL", "UG")):
            asel(v(n_), v("U0", 16 - q, 2064 - q), [[-1, 16], [-1, 128]], q)

    def lanes(t):
        c0 = 896 * t % 2048 // 16
        mms([(v("q2", 0, 128), win("RD2", i), v("TB", i, 2048, 16)) for i in range(16)])
        ts(v("NW", 0, 128 - c0), v("q2", c0, 128), 4096.0, A.is_ge)
        if c0:
            ts(v("NW", 128 - c0, 128), v("q2", 0, c0), 4096.0, A.is_ge)
        mms([(v("q3", 0, 128), v("BO"), v("NW"))])
        mms([(v("q4", 0, 128), v("NW"), v("BO"))])
        mms([(v("q3", 128, 256), v("LPA"), v("NW"))])
        act(v("TTB", 0, 128), v("q4", 0, 128))
        scan(v("CUM"), v("q3", 0, 128), v("ZF"), A.add)
        tt(v("TTB", 256, 384), v("q4", 0, 128), v("EQ0"), A.mult)
        tt(v("TTB", 128, 256), v("q4", 0, 128), v("LT"), A.mult)
        mms([(v("q5", 8, 16), v("TTB", 256, 384), v("RH12", 8, 16))])
        mms([(v("q5", 0, 8), v("TTB", 0, 128), v("RH12", 0, 8)), (v("q5", 0, 8), v("TTB", 128, 256), v("RH12", 8, 16))])
        tt(v("POS"), v("q3", 128, 256), v("CUM"), A.add)
        ts(v("OF", 0, 8), v("q5", 8, 16), 0.5, A.is_lt)
        tt(v("OF", 8, 16), v("OF", 0, 8), v("W8", 0, 8), A.mult)
        tt(v("OF", 16, 24), v("q5", 0, 8), v("OF", 8, 16), A.add)
        cp(v("OFu"), v("OF", 16, 24))
        sca(v("CW"), v("OFu"), v("C1"))
        ts(v("EX", 0, 32), v("JW"), v("CUM", 127, 128), A.is_ge)
        tt(v("EX", 32, 64), v("EX", 0, 32), v("JC", 32, 64), A.mult)
        scan(v("CC"), v("CW", 0, 512), v("ZR"), A.max)
        mms([(v("q5", 32, 64), win("RD0", i), v("CC", i, 512, 16)) for i in range(16)])
        cp(v("CLu"), v("q5", 32, 64))
        gtt(v("OH"), v("POS"), v("CLu"), v("JI"), A.is_equal)
        mms([(v("q6", 0, 32), win("RC", i), v("CC", i, 512, 16)) for i in range(16)],
            [(v("q6", 0, 32), win("RI", i), v("OH", i, 512, 16)) for i in range(16)])
        ts(v("Li", 0, 32), v("q6", 0, 32), float(16 * c0), A.add)
        ts(v("Li", 32, 64), v("Li", 0, 32), 2047, A.bitwise_and)
        tt(v("Li", 0, 32), v("Li", 32, 64), v("EX", 32, 64), A.max)
        cp(v("Lu"), v("Li", 0, 32))

    def fetch(t):
        sgat(v("TBL"), v("TB"), v("Lu"))
        gat(v("Wu"), v("WD"), v("Lu"))
        mms([(v("q5", 64, 96), win("RH", i), v("TBL", i, 512, 16)) for i in range(16)])
        cp(v("STu"), v("q5", 64, 96))
        gat(v("Ku"), v("RQ"), v("STu"))
        sgat(v("KX"), v("RQ"), v("STu"), 8192.0)
        sgat(v("W4"), v("WD"), v("Lu"), 4.0)

    CH = (0, 160, 320, 448, 512)

    def check(t):
        def ch(x, k):
            return v(x, CH[k], CH[k + 1])

        def sig(k):
            sgat(tile("sg", k), v("SG"), ch("Ku", k))

        def tile(x, k, p=None):
            n = 16 * (CH[k + 1] - CH[k])
            name = "%s%d" % (x, k & 1)
            return v(name, 0, n) if p is None else v(name, p, n, 16)

        def typ(k, e):
            (gat if e == "V" else sgat)(tile("hg", k), v("TB"), ch("Wu", k))

        def val(k):
            gtt(tile("mm", k), v("X"), ch("Wu", k), tile("sg", k), A.max)

        def sums(k):
            q, n = ("q0", "q1", "q7", "q0")[k], CH[k + 1] - CH[k]
            parts = [[(v(q, 0, n), win(R, p), tile(x, k, p)) for p in range(16)] for R, x in (("RX", "hg"), ("RN", "sg"), ("R2", "mm"))]
            mms(*(parts if k < 3 else (parts[1], parts[0], parts[2])))

        def small(k):
            q, n = ("q0", "q1", "q7", "q0")[k], CH[k + 1] - CH[k]
            tt(v("ED", 0, n), v(q, 0, n), ch("KX", k), A.subtract)
            ts(v("ED", 160, 160 + n), v("ED", 0, n), 8191, A.bitwise_and)
            tt(v("O0", 0, n), v("ED", 160, 160 + n), v("ED", 0, n), A.not_equal)
            ts(v("GA", 0, n), v("ED", 160, 160 + n), v("thB", 1, 2), A.is_gt, 2.0, A.add)
            tt(v("FT", 512 + CH[k], 512 + CH[k + 1]), v("O0", 0, n), ch("PM", k), A.mult)
            tt(ch("FT", k), v("FT", 512 + CH[k], 512 + CH[k + 1]), v("GA", 0, n), A.mult)
            act(ch("FOf", k), ch("FT", k))

        sig(0)
        typ(0, "V")
        val(0)
        sums(0)
        if t == 0:
            last_constants()
        sig(1)
        typ(1, "S")
        ts(v("PM"), v("Ku"), 1024.0, A.is_lt)
        val(1)
        sums(1)
        sig(2)
        typ(2, "S")
        tt(v("W4K"), v("W4"), v("KX"), A.add)
        small(0)
        mms([(v("q6"), v("BC"), v("CC")), (v("q6"), v("BOI"), v("OH")), (v("q6"), v("UD"), v("TBL"))])
        act(v("P2"), v("q6"), F.Identity, bias=float(896 * t % 2048))
        val(2)
        sums(2)
        sig(3)
        typ(3, "S")
        small(1)
        cp(v("TY", 0, 32), v("q5", 64, 96))
        tt(v("HLi", 0, 32), v("TY", 0, 32), v("TY", 0, 32), A.mult)
        ts(v("HLi", 0, 32), v("HLi", 0, 32), 4, A.arith_shift_right)
        ts(v("HLi", 32, 64), v("TY", 0, 32), 5.0, A.mult)
        tt(v("TY", 32, 64), v("HLi", 0, 32), v("HLi", 32, 64), A.add)
        ms(v("P1W", 0, 192), 0.0)
        ms(v("P2W", 0, 128), 8388608.0)
        ms(v("CW", 0, 512), 0.0)
        val(3)
        sums(3)
        small(2)
        small(3)

    def post(t):
        last = t == 2
        c16 = 896 * t % 2048
        lw = lambda k: v("LW", 32 * k, 32 * k + 32)
        mms([(v("q3", 0, 64), win("R1", i), v("FT", i, 1024, 16)) for i in range(16)])
        ts(lw(0), v("q3", 32, 64), -2.0, A.mult)
        tt(lw(1), v("q3", 0, 32), lw(0), A.add)
        ts(lw(4), lw(0), -1.0, A.is_lt)
        ts(lw(2), lw(1), 0.5, A.is_lt)
        ts(lw(3), lw(1), 3.5, A.is_lt)
        tt(v("RP", 0, 32), lw(3), lw(2), A.subtract)
        tt(v("RP", 32, 64), lw(4), lw(2), A.mult)
        mms([(v("q4", 0, 64), v("BO"), v("RP"))])
        mms([(v("q4", 64, 128), v("LPB"), v("RP"))])
        mm = [(v("q6"), v("X2D"), v("TBL"))]
        tt(v("HLi", 64, 96), v("TY", 32, 64), lw(1), A.add)
        scan(lw(5), v("q4", 0, 32), v("ZF", 0, 32), A.add)
        scan(lw(6), v("q4", 32, 64), v("ZF", 0, 32), A.add)
        ts(v("HLi", 64, 96), v("HLi", 64, 96), 1023, A.bitwise_and)
        tt(v("LW", 224, 288), v("q4", 64, 128), v("LW", 160, 224), A.add)
        ts(v("GM"), lw(2), -8192.0, A.mult)
        tt(v("LW", 288, 352), v("LW", 224, 288), v("LIM"), A.is_lt)
        tt(v("LW", 352, 416), v("LW", 224, 288), v("DD"), A.subtract)
        tt(v("HLi", 64, 96), v("HLi", 64, 96), v("TY", 0, 32), A.subtract)
        tt(v("LW", 352, 416), v("LW", 352, 416), v("LW", 288, 352), A.mult)
        ts(lw(4), lw(3), 0.5, A.is_lt)
        tt(lw(9), lw(11), lw(12), A.add)
        tt(v("HLi", 64, 96), v("HLi", 64, 96), lw(4), A.mult)
        tt(lw(9), lw(9), v("J192"), A.add)
        tt(v("HLi", 64, 96), v("HLi", 64, 96), v("TY", 0, 32), A.add)
        cp(v("PFu"), lw(9))
        op("V", lambda: g.vector.tensor_tensor(ind(v("P1W"), v("PFu")), ap(v("W4K")), ap(v("FOf")), A.add),
           [v("W4K"), v("FOf"), v("PFu")], [v("P1W")], ew(512, 3.5))
        ts(v("HLi", 128, 160), v("HLi", 64, 96), 5, A.arith_shift_right)
        ts(v("HLi", 160, 192), v("HLi", 64, 96), 31, A.bitwise_and)
        cp(v("HLb"), v("HLi", 128, 192))
        ai = lambda lo, hi: v("AI", lo, hi)
        af = lambda lo, hi: v("AF", lo, hi)
        ab = lambda lo, hi: v("AB", lo, hi)
        cp(ai(0, 64), v("P1W", 128, 192))
        ts(ai(64, 128), ai(0, 64), 2, A.bitwise_and)
        ts(ab(0, 64), ai(64, 128), 0.5, A.mult)
        mms([(v("q4", 0, 64), v("TRI"), ab(0, 64))])
        sca(v("P2W"), v("PFu"), v("P2"))
        for i in range(16):
            for U, d in (("UH", v("HLb", 0, 32)), ("UL", v("HLb", 32, 64)), ("UG", v("GM"))):
                mm.append((v("q6", i, 512, 16), v(U, 128 * i, 128 * i + 128), d))
        ts(af(0, 64), v("q4", 0, 64), 0.5, A.is_lt)
        tt(af(0, 64), af(0, 64), ab(0, 64), A.mult)
        tt(af(64, 128), v("P1W", 128, 192), af(0, 64), A.mult)
        mms([(v("q4", 0, 64), v("BOf"), af(64, 128))])
        mms(mm[:1], mm[1:])
        act(v("TBn"), v("q6"), F.Identity, bias=col["b2"])
        bi = lambda k: v("BI", 128 * k, 128 * k + 128)
        cp(bi(0), v("P2W", 0, 128))
        tt(af(216, 280), v("q4", 0, 64), v("EQ0", 0, 64), A.mult)
        cp(ai(128, 192), v("q4", 0, 64))
        tt(af(280, 312), v("AF", 216, 280, 2), v("AF", 217, 280, 2), A.add)
        tt(af(312, 328), v("AF", 280, 312, 2), v("AF", 281, 312, 2), A.add)
        tt(af(328, 336), v("AF", 312, 328, 2), v("AF", 313, 328, 2), A.add)
        tt(ai(192, 196), v("AF", 328, 336, 2), v("AF", 329, 336, 2), A.add)
        ts(bi(1), bi(0), 2047, A.bitwise_and)
        ts(ai(196, 264), ai(128, 196), 2, A.arith_shift_right, 2047, A.bitwise_and)
        cp(af(128, 196), ai(196, 264))
        cp(v("AU", 0, 4), ai(260, 264))
        cp(v("BU", 0, 128), bi(1))
        sgat(ab(320, 384), v("SXT"), v("AU", 0, 4))
        for h in (0, 1):
            sgat(v("sg0", 1024 * h, 1024 * h + 1024), v("X"), v("BU", 64 * h, 64 * h + 64))
        ts(bi(2), bi(0), 12, A.arith_shift_right, 2047, A.bitwise_and)
        for c in range(4):
            ts(ab(64 + 64 * c, 128 + 64 * c), af(128, 192), af(192 + c, 193 + c), A.is_equal)
        tt(bi(3), bi(2), bi(2), A.mult)
        ts(bi(4), bi(2), col["m2"], A.mult, kif, A.add)
        tt(ab(64, 320), ab(64, 320), v("MK"), A.mult)
        ts(bi(3), bi(3), 5, A.arith_shift_right)
        for c in range(4):
            act(ab(64 + 64 * c, 128 + 64 * c), ab(64 + 64 * c, 128 + 64 * c), accum_out=af(200 + c, 201 + c))
        tt(bi(3), bi(3), bi(4), A.add)
        ts(ai(264, 268), ai(192, 196), 2, A.bitwise_and)
        ts(bi(3), bi(3), 2047, A.bitwise_and)
        ts(af(204, 208), af(200, 204), 0.5, A.is_gt)
        ts(af(208, 212), ai(264, 268), 0.5, A.is_lt)
        cp(v("BU", 128, 256), bi(3))
        tt(af(204, 208), af(204, 208), af(208, 212), A.max)
        ts(ai(272, 336), ai(128, 192), 18, A.arith_shift_right)
        tt(af(204, 208), af(204, 208), v("W8", 8, 12), A.mult)
        ts(ai(336, 400), ai(128, 192), 13, A.arith_shift_right, 31, A.bitwise_and)
        tt(af(204, 208), af(204, 208), af(192, 196), A.max)
        cp(ab(384, 512), ai(272, 400))
        cp(v("AU", 4, 8), af(204, 208))
        mms([(v("q2", 0, 64), v("K34"), ab(320, 384)), (v("q2", 0, 64), v("D0"), ab(384, 448)), (v("q2", 0, 64), v("D1"), ab(448, 512))])
        act(ab(512, 576), v("q2", 0, 64), F.Identity, bias=col["b2"])
        sca(v("TB"), v("Lu"), v("TBn"))
        sca(v("TB"), v("AU", 4, 8), ab(512, 576))
        if not last:
            dma("Y", v("FL%d" % (t + 1)), v("TB", 0, 2048, 1, slice(2, 128, 16)))
            send(7 + t, rank - 2 - t, v("FI%d" % (t + 1)), v("FL%d" % (t + 1)))
            arrive(7 + t, v("FI%d" % (t + 1)), 7 + t, 4.0)
            ts(v("EX", 0, 32), v("EX", 0, 32), 0.5, A.is_lt)
            tt(v("EX", 0, 32), v("EX", 0, 32), lw(2), A.mult)
            red(v("thB", 2, 3), v("EX", 0, 32))
            cp(ab(576, 577), v("thB", 2, 3))

    def bsum(t):
        mms([(v("q3", 500, 501), v("ON"), v("AB", 576, 577))])
        cp(v("CN", 0, 1), v("q3", 500, 501))
        ts(v("CN", 1, 2), v("CN", 0, 1), 255, A.bitwise_and)
        tt(v("thB", 1, 2), v("thB", 0, 1), v("CN", 1, 2), A.add)

    def repairs(t):
        bi = lambda k: v("BI", 128 * k, 128 * k + 128)
        bf = lambda lo, hi: v("BF2", lo, hi)
        sm = lambda k: v("BI", 1024 + 8 * k, 1032 + 8 * k)
        xe, c16 = "XE%d" % t, 896 * t % 2048
        mms([(v("q5", 0, 8), win("R0f", i), v("P2W", i, 128, 16)) for i in range(16)])
        for h in (0, 1):
            sgat(v("mm0", 1024 * h, 1024 * h + 1024), v(xe), v("BU", 128 + 64 * h, 192 + 64 * h))
            for b in (2 * h, 2 * h + 1):
                q, lo, hi = "q%d" % (b & 1), 512 * b, 512 * b + 512
                mms([(v(q), v("NI"), v("sg0", lo, hi)), (v(q), v("ID"), v("mm0", lo, hi))])
                act(v("hg0", lo, hi), v(q), F.Abs)
            mms([(v("q7", 64 * h, 64 * h + 64), win("R1", m), v("hg0", 1024 * h + m, 1024 * h + 1024, 16)) for m in range(16)])
        cp(sm(0), v("q5", 0, 8))
        cp(bi(4), v("P1W", 0, 128))
        ts(sm(1), sm(0), 2047, A.bitwise_and)
        ts(sm(2), sm(0), 12, A.arith_shift_right, 2047, A.bitwise_and)
        ts(bi(5), bi(4), 1, A.bitwise_and)
        ts(bi(6), bi(4), 2, A.arith_shift_right, 2047, A.bitwise_and)
        tt(sm(3), sm(2), sm(2), A.mult)
        ts(sm(4), sm(2), 2.0, A.mult, 1.0, A.add)
        ts(sm(3), sm(3), 5, A.arith_shift_right)
        tt(sm(3), sm(3), sm(2), A.add)
        ts(bf(520, 528), sm(0), 8388608.0, A.is_ge)
        ts(bf(0, 128), v("q7", 0, 128), 16.0, A.mult, kif, A.add)
        op("V", lambda: g.vector.transpose(ap(bf(128, 256)), ap(bf(0, 128))), [bf(0, 128)], [bf(128, 256)])
        lo, n, o = 128, 128, 256
        while n > 8:
            tt(bf(o, o + n // 2), v("BF2", lo, lo + n, 2), v("BF2", lo + 1, lo + n, 2), A.min)
            lo, n, o = o, n // 2, o + n // 2
        for s1 in (0, 1):
            mms([(v("q7", 256 + s1, 264, 2), v("SW", 256 * s1 + 128 * g2, 256 * s1 + 128 * g2 + 128), v("BF2", lo + g2, lo + 8, 2)) for g2 in (0, 1)])
        cp(sm(6), v("q7", 256, 264))
        ts(bf(528, 536), v("q7", 256, 264), 65400.0, A.is_gt)
        ts(sm(7), sm(6), 15, A.bitwise_and)
        tt(bf(528, 536), bf(528, 536), bf(520, 528), A.max)
        tt(sm(7), sm(7), sm(4), A.mult)
        tt(bf(528, 536), bf(528, 536), v("W8", 0, 8), A.mult)
        tt(sm(7), sm(7), sm(3), A.add)
        dw = "DW%d" % t
        tt(v(dw, 128, 136), bf(528, 536), sm(1), A.max)
        ts(sm(7), sm(7), 2047, A.bitwise_and)
        cp(v("BU", 264, 272), v(dw, 128, 136))
        cp(v("BU", 256, 264), sm(7))
        gat(bf(384, 512), v("WE%d" % t), v("BU", 256, 264))
        tt(bf(384, 512), bf(384, 512), bi(6), A.subtract)
        tt(bf(384, 512), bf(384, 512), bi(5), A.mult)
        tt(v(dw, 0, 128), bf(384, 512), bi(6), A.add)
        sca(v("WD"), v("BU", 264, 272), v(dw, 0, 128))
        if t == 2:
            fin.append(dma("Y", None, v("WD", 0, 2048), o=T.ym[:]))
            return
        for t2 in range(t + 1, 3):
            slot = 9 + t + t2 - 1
            send(slot, rank - 1 - t2, v("Di%d%d" % (t, t2)), v(dw))
            arrive(slot, v("Di%d%d" % (t, t2)), slot, 4.0)

    def helper(t):
        dma("Y", v("XE%d" % t, 0, 2048, 1, slice(2, 128, 16)), v("FI%d" % t))
        for s in range(t):
            b = "Di%d%d" % (s, t)
            cp(v("BU", 272, 280), v(b, 128, 136))
            sca(v("WE%d" % t), v("BU", 272, 280), v(b, 0, 128))

    def flags_out():
        mms([(v("q2", 0, 128), win("RH", b), v("TB", 128 * b, 128 * b + 128)) for b in range(16)])
        mms([(v("q2", 128, 256), win("RD2", b), v("TB", 128 * b, 128 * b + 128)) for b in range(16)])
        cp(v("CUM"), v("q2", 0, 128))
        ts(v("POS"), v("q2", 128, 256), 4096.0, A.is_lt)
        fin.append(dma("Y", None, v("CUM"), o=T.yh[:]))
        fin.append(dma("Y", None, v("POS"), o=T.yv[:]))

    late_constants()
    for t in range(3):
        lanes(t)
        fetch(t)
        check(t)
        helper(t)
        post(t)
        if t == 2:
            flags_out()
        repairs(t)
        if t < 2:
            bsum(t)
    issue()
    for sem in fin:
        wait("Y", sem, 16, {})
    for sem, n in sent:
        wait("G", sem, n, {})
    for sem in cnt:
        wait("G", sem, cnt[sem], {})
